import numpy as np
import ml_dtypes


def mxq(x, axis, fmt="e4m3"):
    dtype, down = {"e4m3": (ml_dtypes.float8_e4m3fn, 7), "e5m2": (ml_dtypes.float8_e5m2, 14)}[fmt]
    v = np.moveaxis(np.asarray(x, np.float32).astype(ml_dtypes.bfloat16).astype(np.float64), axis, -1)
    blocks = v.reshape(v.shape[:-1] + (-1, 32))
    amax = np.abs(blocks).max(-1, keepdims=True)
    byte = np.maximum(np.where(amax > 0, np.frexp(amax)[1] - 1 + 127, 0) - down, 1)
    scale = np.exp2(byte - 127.0)
    codes = (blocks / scale).astype(np.float32).astype(dtype).astype(np.float64)
    return np.moveaxis((codes * scale).reshape(v.shape), -1, axis)


WIDE = False


def mx_kscale(k):
    if not WIDE:
        return np.ones(k)
    levels = np.array([10, -10, 5, -5, 0])
    if k % 512:
        return np.exp2(np.random.permutation(np.resize(levels, k // 32))).repeat(32)
    a = np.empty((k // 512, 16))
    for p in range(k // 512):
        a[p, :8] = np.random.permutation(np.resize(levels, 8))
        for g in range(8):
            far = levels[np.abs(levels - a[p, g]) >= 10]
            a[p, g + 8] = far[np.random.randint(len(far))]
    return np.exp2(a.ravel()).repeat(32)


def f64(x):
    return np.asarray(x).astype(np.float64)


def striped(idx):
    return np.tile(np.asarray(idx).reshape(-1, 16).T, (8, 1)).astype(np.uint16)


def unstriped(offs):
    return offs[:16].T.reshape(-1).astype(np.int64)


E2M1 = np.array([0.0, 0.5, 1.0, 1.5, 2.0, 3.0, 4.0, 6.0, -0.0, -0.5, -1.0, -1.5, -2.0, -3.0, -4.0, -6.0])


def pack_weight(w, fmt):
    k, n = w.shape
    w = f64(np.asarray(w, np.float32).astype(ml_dtypes.bfloat16)).reshape(k // 32, 32, n)
    amax = np.abs(w).max(1)
    if fmt == "e4m3":
        byte = np.frexp(amax)[1] - 1 + 127 - 7
    else:
        mant, ex = np.frexp(amax / 6.0)
        byte = np.where(mant > 0.5, ex, ex - 1) + 127
    byte = np.clip(np.where(amax > 0, byte, 1), 1, 254)
    scaled = (w * np.exp2(127.0 - byte)[:, None, :]).reshape(k, n).astype(np.float32)
    by_word = np.ascontiguousarray(scaled.reshape(k // 512, 128, 4, n).transpose(0, 1, 3, 2))
    if fmt == "e4m3":
        words = by_word.astype(ml_dtypes.float8_e4m3fn).view(np.uint8)
    else:
        c = by_word.astype(ml_dtypes.float4_e2m1fn).view(np.uint8) & 0xF
        words = (c[..., 0::2] | (c[..., 1::2] << 4)).reshape(k // 512, 128, 2 * n)
    return np.ascontiguousarray(words), np.ascontiguousarray(byte.astype(np.uint8).reshape(k // 512, 16, n))


def unpack_weight(words, scales, fmt):
    g, _, n = scales.shape
    words = np.ascontiguousarray(words).reshape(g, 128, n, -1)
    if fmt == "e4m3":
        vals = words.view(ml_dtypes.float8_e4m3fn).astype(np.float64)
    else:
        nib = np.empty((g, 128, n, 4), np.uint8)
        nib[..., 0::2] = words & 0xF
        nib[..., 1::2] = words >> 4
        vals = E2M1[nib]
    vals = vals * np.repeat(np.exp2(scales.astype(np.float64) - 127.0), 8, axis=1)[..., None]
    return vals.transpose(0, 1, 3, 2).reshape(g * 512, n)


B, N, T, D, DV, NQ = 1, 1024, 2048, 1024, 256, 256
CAP = 2.0


def setup_inputs():
    n = np.random.standard_normal
    idx = np.sort(np.random.permutation(T)[:B * N].reshape(B, N), axis=1).reshape(-1)
    s = mx_kscale(D)[:, None]
    u = np.ones(T)
    u[idx] = mx_kscale(B * N)
    r = np.random.uniform(0.5, 2.0, T)
    k = n((D, T)) / s
    v = n((DV, T)) / (u * r)
    kp = pack_weight(k, "e2m1")
    return {
        "qT": (n((B, D, NQ)) * s * (1.00 / np.sqrt(D))).astype(np.float32),
        "k_words": np.ascontiguousarray(kp[0].reshape(D // 1024, 2, 128, T, 2).transpose(0, 2, 3, 1, 4)).reshape(D // 1024, 128, T, 4),
        "k_scales": kp[1],
        "vT": v.astype(np.float32),
        "vs": np.tile(u * r, (128, 1)).astype(np.float32),
        "offs": striped(idx),
    }


def reference(qT, k_words, k_scales, vT, vs, offs):
    idx = unstriped(offs)
    k = unpack_weight(k_words.reshape(D // 1024, 128, T, 2, 2).transpose(0, 3, 1, 2, 4).reshape(D // 512, 128, 2 * T), k_scales, "e2m1")
    v = f64(vT)
    pick = lambda x: x[:, idx].reshape(x.shape[0], B, N).transpose(1, 0, 2)
    q = f64(qT)
    score = mxq(q, 1, "e4m3").transpose(0, 2, 1) @ pick(k)
    score = CAP * np.tanh(score / CAP)
    p = 1.0 / (1.0 + np.exp(-score))
    w = p * pick(f64(vs))[:, :1, :]
    y = mxq(w, 2, "e4m3") @ mxq(pick(v).transpose(0, 2, 1), 1, "e4m3")
    y = y / 16.0
    return y

@@ -1,0 +1,217 @@
+from contextlib import ExitStack
+
+import concourse.mybir as mybir
+
+N, T, D, DV, NQ = 1024, 2048, 1024, 256, 256
+FLOPS = 2 * NQ * N * D + 2 * NQ * N * DV
+
+F32 = mybir.dt.float32
+BF16 = mybir.dt.bfloat16
+I32 = mybir.dt.int32
+U32 = mybir.dt.uint32
+U16 = mybir.dt.uint16
+U8 = mybir.dt.uint8
+FP8X4 = mybir.dt.float8_e4m3fn_x4
+FP4X4 = mybir.dt.float4_e2m1fn_x4
+ACT = mybir.ActivationFunctionType
+ALU = mybir.AluOpType
+
+P = 128
+PACK = 4
+D_PASSES = D // (P * PACK)
+SLOT_PASSES = N // (P * PACK)
+Q_BLOCKS = NQ // P
+V_BLOCKS = DV // P
+
+
+def tile_attend_sigm_cap_srtq256n1024t2048_kernel(tc, qT, k_words, k_scales, vT, vs, offs, out):
+    nc = tc.nc
+    with ExitStack() as ctx:
+        sb = ctx.enter_context(tc.tile_pool(name="sb", bufs=1))
+        ps = ctx.enter_context(tc.psum_pool(name="ps", bufs=1))
+
+        offsets = sb.tile([P, N // 16], U16, name="offsets")
+        nc.sync.dma_start(offsets[:], offs)
+
+        ks_pool = sb.tile([P, T // 4], I32, name="ks_pool", align_bytes=64)
+        nc.gpsimd.memset(ks_pool[:], 0)
+        blank = sb.tile([P, P], F32, name="blank", tag="keys", align_bytes=64)
+        nc.gpsimd.memset(blank[:], 0.0)
+        ident = sb.tile([P, P], F32, name="ident")
+        nc.gpsimd.affine_select(
+            out=ident[:],
+            in_=blank[:],
+            compare_op=ALU.not_equal,
+            fill=1.0,
+            base=0,
+            pattern=[[-1, P]],
+            channel_multiplier=1,
+        )
+        ks_second = sb.tile([P, N // 4], I32, name="ks_second", align_bytes=64)
+        nc.gpsimd.memset(ks_second[:], 0)
+        zero_in = sb.tile([P, 1], F32, name="zero_in", tag="queries", align_bytes=64)
+        nc.vector.memset(zero_in[:], 0.0)
+        vs_pool = sb.tile([P, T], F32, name="vs_pool", align_bytes=64)
+        nc.vector.memset(vs_pool[:, : T - 1], 0.0)
+        nc.vector.memset(vs_pool[:, T - 1 :], 0.0)
+        zero = sb.tile([P, 1], F32, name="zero")
+        nc.scalar.activation(zero[:], zero_in[:], ACT.Tanh)
+
+        for quad in range(4):
+            nc.sync.dma_start(
+                ks_pool[32 * quad : 32 * quad + 8, :],
+                k_scales[:, 4 * quad : 4 * quad + 4, :].bitcast(I32),
+            )
+        kw_pool = sb.tile([P, T], I32, name="kw_pool", tag="keys", align_bytes=64)
+        kw_dram = k_words[0].rearrange("p t b -> p (t b)").bitcast(I32)
+        for lo, hi in ((0, 1536), (1536, T)):
+            nc.sync.dma_start(kw_pool[:, lo:hi], kw_dram[:, lo:hi])
+        q_raw = sb.tile([P, D_PASSES, PACK, NQ], F32, name="q_raw", tag="queries", align_bytes=64)
+        for o in range(D_PASSES):
+            nc.sync.dma_start(q_raw[:, o], qT[0, o * 512 : (o + 1) * 512, :].rearrange("(p j) q -> p j q", j=PACK))
+        nc.sync.dma_start(vs_pool[0:1, :], vs[0:1, :])
+
+        kw_got = sb.tile([P, PACK, N // PACK], U32, name="kw_got", align_bytes=64)
+        kw_use = sb.tile([P, D_PASSES, PACK, N // PACK], U16, name="kw_use", align_bytes=64)
+
+        def gather_words(g):
+            cols = slice(g * P, (g + 1) * P)
+            reach = T - N + (g + 1) * 512
+            nc.vector.tensor_copy(
+                kw_got[:, :, cols].rearrange("x t n -> x n t"),
+                kw_pool[:, :reach].bitcast(U32).indirect(offsets[:, g * 32 : (g + 1) * 32]),
+            )
+
+        def part_words(g):
+            cols = slice(g * P, (g + 1) * P)
+            nc.vector.tensor_copy(
+                kw_use[:, :, :, cols],
+                kw_got[:, :, cols].bitcast(U16).rearrange("x t (n o) -> x o t n", o=D_PASSES),
+            )
+
+        ks_got = sb.tile([P, N], U8, name="ks_got", tag="values", align_bytes=64)
+        ks_first = sb.tile([P, PACK, N // PACK], U8, name="ks_first", align_bytes=64)
+        nc.vector.tensor_copy(ks_got[:], ks_pool[:].bitcast(U8).indirect(offsets[:]))
+        nc.vector.tensor_copy(ks_first[:], ks_got[:].rearrange("x (n t) -> x t n", t=PACK))
+        both = ks_first[:].rearrange("x t n -> x (t n)").bitcast(I32)
+        for quad in range(4):
+            nc.sync.dma_start(ks_second[32 * quad : 32 * quad + 4, :], both[32 * quad + 4 : 32 * quad + 8, :])
+        ks_use = [ks_first[:], ks_second[:].bitcast(U8).rearrange("x (t n) -> x t n", t=PACK)]
+
+        v_pool = sb.tile([P, V_BLOCKS, T], F32, name="v_pool", tag="values", align_bytes=64)
+        for b in range(V_BLOCKS):
+            nc.sync.dma_start(v_pool[:, b, :], vT[b * P : (b + 1) * P, :])
+
+        for g in range(SLOT_PASSES):
+            gather_words(g)
+            part_words(g)
+
+        q_codes = sb.tile([P, D_PASSES, NQ], U32, name="q_codes", align_bytes=64)
+        q_scales = sb.tile([P, D_PASSES, NQ], U8, name="q_scales", align_bytes=64)
+        for o, lo, hi in ((0, 0, NQ), (1, 0, P), (1, P, NQ)):
+            q_bf = sb.tile([P, hi - lo, PACK], BF16, name=f"q_bf{o}{lo}", align_bytes=64)
+            nc.scalar.copy(q_bf[:], q_raw[:, o, :, lo:hi].rearrange("p j q -> p q j"))
+            nc.vector.quantize_mx(
+                out=q_codes[:, o, lo:hi].bitcast(FP8X4),
+                scales=q_scales[:, o, lo:hi],
+                in_=q_bf[:].rearrange("p q j -> p (q j)"),
+            )
+
+        vs_got = sb.tile([P, N], F32, name="vs_got")
+        nc.vector.tensor_copy(vs_got[:], vs_pool[:].indirect(offsets[:]))
+        vs_half = sb.tile([P, SLOT_PASSES, PACK], F32, name="vs_half")
+        for g in range(SLOT_PASSES):
+            bank = ps.tile([P, PACK, P], F32, name=f"vs_bank{g}", tag=f"edge{g}")
+            for t in range(PACK):
+                nc.tensor.transpose(bank[:, t, :], vs_got[:, 512 * g + t : 512 * (g + 1) : PACK], ident[:])
+            nc.scalar.activation(vs_half[:, g, :], bank[:, :, 0], ACT.Copy, scale=0.5)
+
+        w_codes = sb.tile([P, SLOT_PASSES, NQ], U32, name="w_codes", align_bytes=64)
+        w_scales = sb.tile([P, SLOT_PASSES, NQ], U8, name="w_scales", align_bytes=64)
+        chunks = [(g, h) for h in range(Q_BLOCKS) for g in range(SLOT_PASSES)]
+        capped = {}
+        for g, h in chunks:
+            cols = slice(g * P, (g + 1) * P)
+            qs = slice(h * P, (h + 1) * P)
+            bank = ps.tile([P, PACK, P], F32, name=f"score{g}{h}")
+            for t in range(PACK):
+                for o in range(D_PASSES):
+                    nc.tensor.matmul_mx(
+                        bank[:, t, :],
+                        lhsT=kw_use[:, o, t, cols].bitcast(FP4X4),
+                        lhsT_scale=ks_use[o][:, t, cols],
+                        rhs=q_codes[:, o, qs].bitcast(FP8X4),
+                        rhs_scale=q_scales[:, o, qs],
+                        start=(o == 0),
+                        stop=(o == D_PASSES - 1),
+                    )
+            inner = sb.tile([P, P, PACK], F32, name=f"inner{g}{h}")
+            nc.scalar.activation(inner[:], bank[:].rearrange("p t q -> p q t"), ACT.Tanh, bias=zero[:], scale=0.5)
+            outer = sb.tile([P, P, PACK], F32, name=f"outer{g}{h}")
+            nc.scalar.activation(outer[:], inner[:], ACT.Tanh, bias=zero[:])
+            capped[g, h] = outer
+
+        v_codes = sb.tile([P, SLOT_PASSES, DV], U32, name="v_codes", align_bytes=64)
+        v_scales = sb.tile([P, SLOT_PASSES, DV], U8, name="v_scales", align_bytes=64)
+        v_words = sb.tile([P, SLOT_PASSES, DV, 2], F32, name="v_words", align_bytes=64)
+
+        def values(b):
+            got = sb.tile([P, 2, N // PACK, 2], BF16, name=f"v_got{b}", align_bytes=64)
+            nc.vector.tensor_copy(got[:].rearrange("e u n s -> e n u s"), v_pool[:, b, :].indirect(offsets[:]))
+            words = got[:].rearrange("e u n s -> e u (n s)").bitcast(F32)
+            bank = ps.tile([P, SLOT_PASSES, 2, P], F32, name=f"v_bank{b}")
+            for g in range(SLOT_PASSES):
+                for u in range(2):
+                    nc.tensor.transpose(bank[:, g, u, :], words[:, u, g * P : (g + 1) * P], ident[:])
+            es = slice(b * P, (b + 1) * P)
+            nc.scalar.copy(v_words[:, :, es, :], bank[:].rearrange("p g u e -> p g e u"))
+            for g in range(SLOT_PASSES):
+                nc.vector.quantize_mx(
+                    out=v_codes[:, g, es].bitcast(FP8X4),
+                    scales=v_scales[:, g, es],
+                    in_=v_words[:, g, es, :].rearrange("p e u -> p (e u)").bitcast(BF16),
+                )
+
+        def weights(g, h):
+            qs = slice(h * P, (h + 1) * P)
+            w_bf = sb.tile([P, P, PACK], BF16, name=f"w_bf{g}{h}", align_bytes=64)
+            nc.vector.scalar_tensor_tensor(
+                w_bf[:],
+                capped[g, h][:],
+                1.0,
+                vs_half[:, g, :].unsqueeze(1).to_broadcast([P, P, PACK]),
+                ALU.add,
+                ALU.mult,
+            )
+            nc.vector.quantize_mx(
+                out=w_codes[:, g, qs].bitcast(FP8X4),
+                scales=w_scales[:, g, qs],
+                in_=w_bf[:].rearrange("p q t -> p (q t)"),
+            )
+
+        values(0)
+        weights(*chunks[0])
+        values(1)
+        for g, h in chunks[1:]:
+            weights(g, h)
+
+        result = [sb.tile([P, DV], F32, name=f"result{h}") for h in range(Q_BLOCKS)]
+        for h in range(Q_BLOCKS):
+            qs = slice(h * P, (h + 1) * P)
+            acc = ps.tile([P, DV], F32, name=f"acc{h}", tag=f"edge{h}")
+            for g in range(SLOT_PASSES):
+                nc.tensor.matmul_mx(
+                    acc[:],
+                    lhsT=w_codes[:, g, qs].bitcast(FP8X4),
+                    lhsT_scale=w_scales[:, g, qs],
+                    rhs=v_codes[:, g, :].bitcast(FP8X4),
+                    rhs_scale=v_scales[:, g, :],
+                    start=(g == 0),
+                    stop=(g == SLOT_PASSES - 1),
+                )
+            if h == 0:
+                nc.scalar.activation(result[h][:], acc[:], ACT.Copy, scale=1.0 / 16.0)
+                nc.scalar.dma_start(out[0, qs, :], result[h][:])
+            else:
+                nc.vector.tensor_scalar_mul(result[h][:], acc[:], 1.0 / 16.0)
+                nc.sync.dma_start(out[0, qs, :], result[h][:])

@@ -18,8 +18,9 @@ ALU = mybir.AluOpType
 
 P = 128
 PACK = 4
-D_PASSES = D // (P * PACK)
-SLOT_PASSES = N // (P * PACK)
+K_PASS = P * PACK
+D_PASSES = D // K_PASS
+SLOT_PASSES = N // K_PASS
 Q_BLOCKS = NQ // P
 V_BLOCKS = DV // P
 
@@ -33,9 +34,19 @@ def tile_attend_sigm_cap_srtq256n1024t2048_kernel(tc, qT, k_words, k_scales, vT,
         offsets = sb.tile([P, N // 16], U16, name="offsets")
         nc.sync.dma_start(offsets[:], offs)
 
-        ks_pool = sb.tile([P, T // 4], I32, name="ks_pool", align_bytes=64)
-        nc.gpsimd.memset(ks_pool[:], 0)
-        blank = sb.tile([P, P], F32, name="blank", tag="keys", align_bytes=64)
+        ks_pool = sb.tile([P, T // 4], I32, name="ks_pool", tag="values0", align_bytes=64)
+        nc.sync.dma_start(ks_pool[96:128, :], k_scales.rearrange("o f t -> f o t").bitcast(I32))
+        kw_pool = sb.tile([P, T], I32, name="kw_pool", align_bytes=64)
+        kw_dram = k_words[0].rearrange("p t b -> p (t b)").bitcast(I32)
+        for lo, hi in ((0, 1536), (1536, T)):
+            nc.sync.dma_start(kw_pool[:, lo:hi], kw_dram[:, lo:hi])
+        q_raw = [sb.tile([P, PACK, NQ], F32, name=f"q_raw{o}", align_bytes=64) for o in range(D_PASSES)]
+        for o in range(D_PASSES):
+            nc.sync.dma_start(q_raw[o][:], qT[0, o * K_PASS : (o + 1) * K_PASS, :].rearrange("(p j) q -> p j q", j=PACK))
+
+        vs_pool = sb.tile([P, T], F32, name="vs_pool", align_bytes=64)
+        nc.gpsimd.memset(vs_pool[:], 0.0)
+        blank = sb.tile([P, P], F32, name="blank")
         nc.gpsimd.memset(blank[:], 0.0)
         ident = sb.tile([P, P], F32, name="ident")
         nc.gpsimd.affine_select(
@@ -47,171 +58,156 @@ def tile_attend_sigm_cap_srtq256n1024t2048_kernel(tc, qT, k_words, k_scales, vT,
             pattern=[[-1, P]],
             channel_multiplier=1,
         )
-        ks_second = sb.tile([P, N // 4], I32, name="ks_second", align_bytes=64)
-        nc.gpsimd.memset(ks_second[:], 0)
-        zero_in = sb.tile([P, 1], F32, name="zero_in", tag="queries", align_bytes=64)
+        zero_in = sb.tile([P, 1], F32, name="zero_in")
         nc.vector.memset(zero_in[:], 0.0)
-        vs_pool = sb.tile([P, T], F32, name="vs_pool", align_bytes=64)
-        nc.vector.memset(vs_pool[:, : T - 1], 0.0)
-        nc.vector.memset(vs_pool[:, T - 1 :], 0.0)
         zero = sb.tile([P, 1], F32, name="zero")
         nc.scalar.activation(zero[:], zero_in[:], ACT.Tanh)
 
-        for quad in range(4):
-            nc.sync.dma_start(
-                ks_pool[32 * quad : 32 * quad + 8, :],
-                k_scales[:, 4 * quad : 4 * quad + 4, :].bitcast(I32),
-            )
-        kw_pool = sb.tile([P, T], I32, name="kw_pool", tag="keys", align_bytes=64)
-        kw_dram = k_words[0].rearrange("p t b -> p (t b)").bitcast(I32)
-        for lo, hi in ((0, 1536), (1536, T)):
-            nc.sync.dma_start(kw_pool[:, lo:hi], kw_dram[:, lo:hi])
-        q_raw = sb.tile([P, D_PASSES, PACK, NQ], F32, name="q_raw", tag="queries", align_bytes=64)
-        for o in range(D_PASSES):
-            nc.sync.dma_start(q_raw[:, o], qT[0, o * 512 : (o + 1) * 512, :].rearrange("(p j) q -> p j q", j=PACK))
+        nc.vector.memset(ks_pool[0:96, :], 0)
+        ks_use = sb.tile([P, D_PASSES, N // 4], I32, name="ks_use", align_bytes=64)
+        nc.vector.memset(ks_use[:], 0)
         nc.sync.dma_start(vs_pool[0:1, :], vs[0:1, :])
 
-        kw_got = sb.tile([P, PACK, N // PACK], U32, name="kw_got", align_bytes=64)
-        kw_use = sb.tile([P, D_PASSES, PACK, N // PACK], U16, name="kw_use", align_bytes=64)
-
-        def gather_words(g):
-            cols = slice(g * P, (g + 1) * P)
-            reach = T - N + (g + 1) * 512
-            nc.vector.tensor_copy(
-                kw_got[:, :, cols].rearrange("x t n -> x n t"),
-                kw_pool[:, :reach].bitcast(U32).indirect(offsets[:, g * 32 : (g + 1) * 32]),
-            )
-
-        def part_words(g):
-            cols = slice(g * P, (g + 1) * P)
-            nc.vector.tensor_copy(
-                kw_use[:, :, :, cols],
-                kw_got[:, :, cols].bitcast(U16).rearrange("x t (n o) -> x o t n", o=D_PASSES),
-            )
-
-        ks_got = sb.tile([P, N], U8, name="ks_got", tag="values", align_bytes=64)
-        ks_first = sb.tile([P, PACK, N // PACK], U8, name="ks_first", align_bytes=64)
+        ks_got = sb.tile([P, N], U8, name="ks_got", align_bytes=64)
         nc.vector.tensor_copy(ks_got[:], ks_pool[:].bitcast(U8).indirect(offsets[:]))
-        nc.vector.tensor_copy(ks_first[:], ks_got[:].rearrange("x (n t) -> x t n", t=PACK))
-        both = ks_first[:].rearrange("x t n -> x (t n)").bitcast(I32)
         for quad in range(4):
-            nc.sync.dma_start(ks_second[32 * quad : 32 * quad + 4, :], both[32 * quad + 4 : 32 * quad + 8, :])
-        ks_use = [ks_first[:], ks_second[:].bitcast(U8).rearrange("x (t n) -> x t n", t=PACK)]
+            nc.sync.dma_start(
+                ks_use[32 * quad : 32 * quad + 4, :, :],
+                ks_got[96 + 8 * quad : 104 + 8 * quad, :].bitcast(I32),
+            )
+        ks_bytes = ks_use[:].rearrange("x o n -> x (o n)").bitcast(U8)
 
-        v_pool = sb.tile([P, V_BLOCKS, T], F32, name="v_pool", tag="values", align_bytes=64)
+        v_pool = [sb.tile([P, T], F32, name=f"v_pool{b}", tag=f"values{b}", align_bytes=64) for b in range(V_BLOCKS)]
         for b in range(V_BLOCKS):
-            nc.sync.dma_start(v_pool[:, b, :], vT[b * P : (b + 1) * P, :])
+            nc.sync.dma_start(v_pool[b][:], vT[b * P : (b + 1) * P, :])
 
+        kw_use = []
         for g in range(SLOT_PASSES):
-            gather_words(g)
-            part_words(g)
+            reach = T - N + (g + 1) * K_PASS
+            kw_got = sb.tile([P, K_PASS], U32, name=f"kw_got{g}", align_bytes=64)
+            nc.vector.tensor_copy(
+                kw_got[:], kw_pool[:, :reach].bitcast(U32).indirect(offsets[:, g * 32 : (g + 1) * 32])
+            )
+            parted = sb.tile([P, D_PASSES, K_PASS], U16, name=f"kw_use{g}", align_bytes=64)
+            nc.vector.tensor_copy(parted[:], kw_got[:].bitcast(U16).rearrange("x (n o) -> x o n", o=D_PASSES))
+            kw_use.append(parted)
 
         q_codes = sb.tile([P, D_PASSES, NQ], U32, name="q_codes", align_bytes=64)
         q_scales = sb.tile([P, D_PASSES, NQ], U8, name="q_scales", align_bytes=64)
-        for o, lo, hi in ((0, 0, NQ), (1, 0, P), (1, P, NQ)):
-            q_bf = sb.tile([P, hi - lo, PACK], BF16, name=f"q_bf{o}{lo}", align_bytes=64)
-            nc.scalar.copy(q_bf[:], q_raw[:, o, :, lo:hi].rearrange("p j q -> p q j"))
+        for o in range(D_PASSES):
+            q_bf = sb.tile([P, NQ, PACK], BF16, name=f"q_bf{o}", align_bytes=64)
+            nc.scalar.copy(q_bf[:], q_raw[o][:].rearrange("p j q -> p q j"))
             nc.vector.quantize_mx(
-                out=q_codes[:, o, lo:hi].bitcast(FP8X4),
-                scales=q_scales[:, o, lo:hi],
+                out=q_codes[:, o, :].bitcast(FP8X4),
+                scales=q_scales[:, o, :],
                 in_=q_bf[:].rearrange("p q j -> p (q j)"),
             )
 
         vs_got = sb.tile([P, N], F32, name="vs_got")
         nc.vector.tensor_copy(vs_got[:], vs_pool[:].indirect(offsets[:]))
-        vs_half = sb.tile([P, SLOT_PASSES, PACK], F32, name="vs_half")
+        vs_col = [sb.tile([P, PACK], F32, name=f"vs_col{g}") for g in range(SLOT_PASSES)]
         for g in range(SLOT_PASSES):
-            bank = ps.tile([P, PACK, P], F32, name=f"vs_bank{g}", tag=f"edge{g}")
-            for t in range(PACK):
-                nc.tensor.transpose(bank[:, t, :], vs_got[:, 512 * g + t : 512 * (g + 1) : PACK], ident[:])
-            nc.scalar.activation(vs_half[:, g, :], bank[:, :, 0], ACT.Copy, scale=0.5)
+            nc.sync.dma_start(vs_col[g][:], vs_got[0:1, g * K_PASS : (g + 1) * K_PASS])
 
-        w_codes = sb.tile([P, SLOT_PASSES, NQ], U32, name="w_codes", align_bytes=64)
-        w_scales = sb.tile([P, SLOT_PASSES, NQ], U8, name="w_scales", align_bytes=64)
         chunks = [(g, h) for h in range(Q_BLOCKS) for g in range(SLOT_PASSES)]
-        capped = {}
+        turned = {}
         for g, h in chunks:
-            cols = slice(g * P, (g + 1) * P)
             qs = slice(h * P, (h + 1) * P)
-            bank = ps.tile([P, PACK, P], F32, name=f"score{g}{h}")
-            for t in range(PACK):
-                for o in range(D_PASSES):
-                    nc.tensor.matmul_mx(
-                        bank[:, t, :],
-                        lhsT=kw_use[:, o, t, cols].bitcast(FP4X4),
-                        lhsT_scale=ks_use[o][:, t, cols],
-                        rhs=q_codes[:, o, qs].bitcast(FP8X4),
-                        rhs_scale=q_scales[:, o, qs],
-                        start=(o == 0),
-                        stop=(o == D_PASSES - 1),
-                    )
-            inner = sb.tile([P, P, PACK], F32, name=f"inner{g}{h}")
-            nc.scalar.activation(inner[:], bank[:].rearrange("p t q -> p q t"), ACT.Tanh, bias=zero[:], scale=0.5)
-            outer = sb.tile([P, P, PACK], F32, name=f"outer{g}{h}")
+            bank = ps.tile([P, K_PASS], F32, name=f"score{g}{h}", tag=f"score{g}{h}")
+            for o in range(D_PASSES):
+                nc.tensor.matmul_mx(
+                    bank[:],
+                    lhsT=q_codes[:, o, qs].bitcast(FP8X4),
+                    lhsT_scale=q_scales[:, o, qs],
+                    rhs=kw_use[g][:, o, :].bitcast(FP4X4),
+                    rhs_scale=ks_bytes[:, o * N + g * K_PASS : o * N + (g + 1) * K_PASS],
+                    start=(o == 0),
+                    stop=(o == D_PASSES - 1),
+                )
+            inner = sb.tile([P, PACK, P], F32, name=f"inner{g}{h}")
+            nc.scalar.activation(
+                inner[:].rearrange("q t p -> q p t"),
+                bank[:].rearrange("q (p t) -> q p t", t=PACK),
+                ACT.Tanh,
+                bias=zero[:],
+                scale=0.5,
+            )
+            outer = sb.tile([P, PACK, P], F32, name=f"outer{g}{h}")
             nc.scalar.activation(outer[:], inner[:], ACT.Tanh, bias=zero[:])
-            capped[g, h] = outer
+            flip = ps.tile([P, PACK, P], F32, name=f"flip{g}{h}", tag=(f"turn{g}" if h == 0 else f"score{g}0"))
+            for t in range(PACK):
+                nc.tensor.transpose(flip[:, t, :], outer[:, t, :], ident[:])
+            turned[g, h] = flip
 
-        v_codes = sb.tile([P, SLOT_PASSES, DV], U32, name="v_codes", align_bytes=64)
-        v_scales = sb.tile([P, SLOT_PASSES, DV], U8, name="v_scales", align_bytes=64)
-        v_words = sb.tile([P, SLOT_PASSES, DV, 2], F32, name="v_words", align_bytes=64)
+        v_codes = sb.tile([P, V_BLOCKS, SLOT_PASSES, P], U32, name="v_codes", align_bytes=64)
+        v_scales = sb.tile([P, V_BLOCKS, SLOT_PASSES, P], U8, name="v_scales", align_bytes=64)
 
         def values(b):
-            got = sb.tile([P, 2, N // PACK, 2], BF16, name=f"v_got{b}", align_bytes=64)
-            nc.vector.tensor_copy(got[:].rearrange("e u n s -> e n u s"), v_pool[:, b, :].indirect(offsets[:]))
-            words = got[:].rearrange("e u n s -> e u (n s)").bitcast(F32)
+            got = sb.tile([P, N], BF16, name=f"v_got{b}", align_bytes=64)
+            nc.vector.tensor_copy(got[:], v_pool[b][:].indirect(offsets[:]))
+            words = got[:].bitcast(F32)
             bank = ps.tile([P, SLOT_PASSES, 2, P], F32, name=f"v_bank{b}")
             for g in range(SLOT_PASSES):
                 for u in range(2):
-                    nc.tensor.transpose(bank[:, g, u, :], words[:, u, g * P : (g + 1) * P], ident[:])
-            es = slice(b * P, (b + 1) * P)
-            nc.scalar.copy(v_words[:, :, es, :], bank[:].rearrange("p g u e -> p g e u"))
-            for g in range(SLOT_PASSES):
-                nc.vector.quantize_mx(
-                    out=v_codes[:, g, es].bitcast(FP8X4),
-                    scales=v_scales[:, g, es],
-                    in_=v_words[:, g, es, :].rearrange("p e u -> p (e u)").bitcast(BF16),
-                )
+                    nc.tensor.transpose(bank[:, g, u, :], words[:, 256 * g + u : 256 * (g + 1) : 2], ident[:])
+            v_words = sb.tile([P, SLOT_PASSES, P, 2], F32, name=f"v_words{b}", align_bytes=64)
+            nc.scalar.copy(v_words[:], bank[:].rearrange("p g u e -> p g e u"))
+            return v_words
+
+        def quantise_values(b, v_words):
+            nc.vector.quantize_mx(
+                out=v_codes[:, b].rearrange("p g e -> p (g e)").bitcast(FP8X4),
+                scales=v_scales[:, b].rearrange("p g e -> p (g e)"),
+                in_=v_words[:].rearrange("p g e u -> p (g e u)").bitcast(BF16),
+            )
+
+        v_turned = [values(b) for b in range(V_BLOCKS)]
+        w_bf = sb.tile([P, Q_BLOCKS, SLOT_PASSES, P, PACK], BF16, name="w_bf", tag="values1", align_bytes=64)
+        w_codes = sb.tile([P, Q_BLOCKS, SLOT_PASSES, P], U32, name="w_codes", align_bytes=64)
+        w_scales = sb.tile([P, Q_BLOCKS, SLOT_PASSES, P], U8, name="w_scales", align_bytes=64)
 
         def weights(g, h):
-            qs = slice(h * P, (h + 1) * P)
-            w_bf = sb.tile([P, P, PACK], BF16, name=f"w_bf{g}{h}", align_bytes=64)
             nc.vector.scalar_tensor_tensor(
-                w_bf[:],
-                capped[g, h][:],
+                w_bf[:, h, g],
+                turned[g, h][:].rearrange("p t q -> p q t"),
                 1.0,
-                vs_half[:, g, :].unsqueeze(1).to_broadcast([P, P, PACK]),
+                vs_col[g][:].unsqueeze(1).to_broadcast([P, P, PACK]),
                 ALU.add,
                 ALU.mult,
             )
+
+        def quantise_weights(g, h):
             nc.vector.quantize_mx(
-                out=w_codes[:, g, qs].bitcast(FP8X4),
-                scales=w_scales[:, g, qs],
-                in_=w_bf[:].rearrange("p q t -> p (q t)"),
+                out=w_codes[:, h, g].bitcast(FP8X4),
+                scales=w_scales[:, h, g],
+                in_=w_bf[:, h, g].rearrange("p q t -> p (q t)"),
             )
 
-        values(0)
-        weights(*chunks[0])
-        values(1)
-        for g, h in chunks[1:]:
-            weights(g, h)
+        quantise_values(0, v_turned[0])
+        weights(0, 0)
+        weights(1, 0)
+        quantise_weights(0, 0)
+        quantise_values(1, v_turned[1])
+        quantise_weights(1, 0)
+        weights(0, 1)
+        weights(1, 1)
+        quantise_weights(0, 1)
+        quantise_weights(1, 1)
 
-        result = [sb.tile([P, DV], F32, name=f"result{h}") for h in range(Q_BLOCKS)]
         for h in range(Q_BLOCKS):
             qs = slice(h * P, (h + 1) * P)
-            acc = ps.tile([P, DV], F32, name=f"acc{h}", tag=f"edge{h}")
-            for g in range(SLOT_PASSES):
-                nc.tensor.matmul_mx(
-                    acc[:],
-                    lhsT=w_codes[:, g, qs].bitcast(FP8X4),
-                    lhsT_scale=w_scales[:, g, qs],
-                    rhs=v_codes[:, g, :].bitcast(FP8X4),
-                    rhs_scale=v_scales[:, g, :],
-                    start=(g == 0),
-                    stop=(g == SLOT_PASSES - 1),
-                )
-            if h == 0:
-                nc.scalar.activation(result[h][:], acc[:], ACT.Copy, scale=1.0 / 16.0)
-                nc.scalar.dma_start(out[0, qs, :], result[h][:])
-            else:
-                nc.vector.tensor_scalar_mul(result[h][:], acc[:], 1.0 / 16.0)
-                nc.sync.dma_start(out[0, qs, :], result[h][:])
+            acc = ps.tile([P, V_BLOCKS, P], F32, name=f"acc{h}", tag=f"score{h}1")
+            for b in range(V_BLOCKS):
+                for g in range(SLOT_PASSES):
+                    nc.tensor.matmul_mx(
+                        acc[:, b, :],
+                        lhsT=w_codes[:, h, g].bitcast(FP8X4),
+                        lhsT_scale=w_scales[:, h, g],
+                        rhs=v_codes[:, b, g].bitcast(FP8X4),
+                        rhs_scale=v_scales[:, b, g],
+                        start=(g == 0),
+                        stop=(g == SLOT_PASSES - 1),
+                    )
+            result = sb.tile([P, DV], F32, name=f"result{h}")
+            nc.scalar.activation(result[:], acc[:].rearrange("q b e -> q (b e)"), ACT.Copy, scale=1.0 / 32.0)
+            nc.sync.dma_start(out[0, qs, :], result[:])

@@ -29,23 +29,23 @@ def tile_attend_sigm_cap_srtq256n1024t2048_kernel(tc, qT, k_words, k_scales, vT,
     nc = tc.nc
     with ExitStack() as ctx:
         sb = ctx.enter_context(tc.tile_pool(name="sb", bufs=1))
+        shared = ctx.enter_context(tc.tile_pool(name="shared", bufs=1))
         ps = ctx.enter_context(tc.psum_pool(name="ps", bufs=1))
 
         offsets = sb.tile([P, N // 16], U16, name="offsets")
         nc.sync.dma_start(offsets[:], offs)
 
-        ks_pool = sb.tile([P, T // 4], I32, name="ks_pool", tag="values0", align_bytes=64)
+        ks_pool = sb.tile([P, T // 4], I32, name="ks_pool", align_bytes=64)
         nc.sync.dma_start(ks_pool[96:128, :], k_scales.rearrange("o f t -> f o t").bitcast(I32))
-        kw_pool = sb.tile([P, T], I32, name="kw_pool", align_bytes=64)
-        kw_dram = k_words[0].rearrange("p t b -> p (t b)").bitcast(I32)
-        for lo, hi in ((0, 1536), (1536, T)):
-            nc.sync.dma_start(kw_pool[:, lo:hi], kw_dram[:, lo:hi])
-        q_raw = [sb.tile([P, PACK, NQ], F32, name=f"q_raw{o}", align_bytes=64) for o in range(D_PASSES)]
-        for o in range(D_PASSES):
-            nc.sync.dma_start(q_raw[o][:], qT[0, o * K_PASS : (o + 1) * K_PASS, :].rearrange("(p j) q -> p j q", j=PACK))
+        v_first = sb.tile([P, T], F32, name="v_first", align_bytes=64)
+        halves = [slice(0, T // 2), slice(T // 2, T)]
+        for cols in halves:
+            nc.sync.dma_start(v_first[:, cols], vT[0:P, cols])
 
         vs_pool = sb.tile([P, T], F32, name="vs_pool", align_bytes=64)
-        nc.gpsimd.memset(vs_pool[:], 0.0)
+        nc.gpsimd.memset(vs_pool[:, halves[0]], 0.0)
+        nc.vector.memset(vs_pool[:, halves[1]], 0.0)
+        nc.sync.dma_start(vs_pool[0:1, :], vs[0:1, :])
         blank = sb.tile([P, P], F32, name="blank")
         nc.gpsimd.memset(blank[:], 0.0)
         ident = sb.tile([P, P], F32, name="ident")
@@ -62,11 +62,17 @@ def tile_attend_sigm_cap_srtq256n1024t2048_kernel(tc, qT, k_words, k_scales, vT,
         nc.vector.memset(zero_in[:], 0.0)
         zero = sb.tile([P, 1], F32, name="zero")
         nc.scalar.activation(zero[:], zero_in[:], ACT.Tanh)
-
         nc.vector.memset(ks_pool[0:96, :], 0)
         ks_use = sb.tile([P, D_PASSES, N // 4], I32, name="ks_use", align_bytes=64)
-        nc.vector.memset(ks_use[:], 0)
-        nc.sync.dma_start(vs_pool[0:1, :], vs[0:1, :])
+        nc.gpsimd.memset(ks_use[:], 0)
+
+        kw_pool = sb.tile([P, T], I32, name="kw_pool", align_bytes=64)
+        kw_dram = k_words[0].rearrange("p t b -> p (t b)").bitcast(I32)
+        q_raw = sb.tile([P, D_PASSES, PACK, NQ], F32, name="q_raw", tag="queries", align_bytes=64)
+        nc.sync.dma_start(kw_pool[:, :1536], kw_dram[:, :1536])
+        for o in range(D_PASSES):
+            nc.sync.dma_start(q_raw[:, o], qT[0, o * K_PASS : (o + 1) * K_PASS, :].rearrange("(p j) q -> p j q", j=PACK))
+        nc.sync.dma_start(kw_pool[:, 1536:], kw_dram[:, 1536:])
 
         ks_got = sb.tile([P, N], U8, name="ks_got", align_bytes=64)
         nc.vector.tensor_copy(ks_got[:], ks_pool[:].bitcast(U8).indirect(offsets[:]))
@@ -77,31 +83,8 @@ def tile_attend_sigm_cap_srtq256n1024t2048_kernel(tc, qT, k_words, k_scales, vT,
             )
         ks_bytes = ks_use[:].rearrange("x o n -> x (o n)").bitcast(U8)
 
-        v_pool = [sb.tile([P, T], F32, name=f"v_pool{b}", tag=f"values{b}", align_bytes=64) for b in range(V_BLOCKS)]
-        for b in range(V_BLOCKS):
-            nc.sync.dma_start(v_pool[b][:], vT[b * P : (b + 1) * P, :])
-
-        kw_use = []
-        for g in range(SLOT_PASSES):
-            reach = T - N + (g + 1) * K_PASS
-            kw_got = sb.tile([P, K_PASS], U32, name=f"kw_got{g}", align_bytes=64)
-            nc.vector.tensor_copy(
-                kw_got[:], kw_pool[:, :reach].bitcast(U32).indirect(offsets[:, g * 32 : (g + 1) * 32])
-            )
-            parted = sb.tile([P, D_PASSES, K_PASS], U16, name=f"kw_use{g}", align_bytes=64)
-            nc.vector.tensor_copy(parted[:], kw_got[:].bitcast(U16).rearrange("x (n o) -> x o n", o=D_PASSES))
-            kw_use.append(parted)
-
-        q_codes = sb.tile([P, D_PASSES, NQ], U32, name="q_codes", align_bytes=64)
-        q_scales = sb.tile([P, D_PASSES, NQ], U8, name="q_scales", align_bytes=64)
-        for o in range(D_PASSES):
-            q_bf = sb.tile([P, NQ, PACK], BF16, name=f"q_bf{o}", align_bytes=64)
-            nc.scalar.copy(q_bf[:], q_raw[o][:].rearrange("p j q -> p q j"))
-            nc.vector.quantize_mx(
-                out=q_codes[:, o, :].bitcast(FP8X4),
-                scales=q_scales[:, o, :],
-                in_=q_bf[:].rearrange("p q j -> p (q j)"),
-            )
+        v_second = sb.tile([P, T], F32, name="v_second", align_bytes=64)
+        nc.sync.dma_start(v_second[:], vT[P : 2 * P, :])
 
         vs_got = sb.tile([P, N], F32, name="vs_got")
         nc.vector.tensor_copy(vs_got[:], vs_pool[:].indirect(offsets[:]))
@@ -109,50 +92,39 @@ def tile_attend_sigm_cap_srtq256n1024t2048_kernel(tc, qT, k_words, k_scales, vT,
         for g in range(SLOT_PASSES):
             nc.sync.dma_start(vs_col[g][:], vs_got[0:1, g * K_PASS : (g + 1) * K_PASS])
 
-        chunks = [(g, h) for h in range(Q_BLOCKS) for g in range(SLOT_PASSES)]
-        turned = {}
-        for g, h in chunks:
-            qs = slice(h * P, (h + 1) * P)
-            bank = ps.tile([P, K_PASS], F32, name=f"score{g}{h}", tag=f"score{g}{h}")
-            for o in range(D_PASSES):
-                nc.tensor.matmul_mx(
-                    bank[:],
-                    lhsT=q_codes[:, o, qs].bitcast(FP8X4),
-                    lhsT_scale=q_scales[:, o, qs],
-                    rhs=kw_use[g][:, o, :].bitcast(FP4X4),
-                    rhs_scale=ks_bytes[:, o * N + g * K_PASS : o * N + (g + 1) * K_PASS],
-                    start=(o == 0),
-                    stop=(o == D_PASSES - 1),
-                )
-            inner = sb.tile([P, PACK, P], F32, name=f"inner{g}{h}")
-            nc.scalar.activation(
-                inner[:].rearrange("q t p -> q p t"),
-                bank[:].rearrange("q (p t) -> q p t", t=PACK),
-                ACT.Tanh,
-                bias=zero[:],
-                scale=0.5,
+        v_bf = sb.tile([P, T], BF16, name="v_bf", align_bytes=64)
+        for cols in halves:
+            nc.scalar.activation(v_bf[:, cols], v_first[:, cols], ACT.Copy)
+
+        q_codes = sb.tile([P, D_PASSES, NQ], U32, name="q_codes", align_bytes=64)
+        q_scales = sb.tile([P, D_PASSES, NQ], U8, name="q_scales", align_bytes=64)
+        q_bf = shared.tile([P, D_PASSES, NQ, PACK], BF16, name="q_bf", offset=0, align_bytes=64)
+        woven = [q_bf[:, o].rearrange("p (c i) j -> p c j i", i=PACK) for o in range(D_PASSES)]
+        rows = [q_raw[:, o].rearrange("p j (c i) -> p c j i", i=PACK) for o in range(D_PASSES)]
+        nc.scalar.copy(woven[0], rows[0])
+        nc.vector.tensor_copy(woven[1], rows[1])
+        for o in range(D_PASSES):
+            nc.vector.quantize_mx(
+                out=q_codes[:, o].bitcast(FP8X4),
+                scales=q_scales[:, o],
+                in_=q_bf[:, o].rearrange("p q j -> p (q j)"),
             )
-            outer = sb.tile([P, PACK, P], F32, name=f"outer{g}{h}")
-            nc.scalar.activation(outer[:], inner[:], ACT.Tanh, bias=zero[:])
-            flip = ps.tile([P, PACK, P], F32, name=f"flip{g}{h}", tag=(f"turn{g}" if h == 0 else f"score{g}0"))
-            for t in range(PACK):
-                nc.tensor.transpose(flip[:, t, :], outer[:, t, :], ident[:])
-            turned[g, h] = flip
 
-        v_codes = sb.tile([P, V_BLOCKS, SLOT_PASSES, P], U32, name="v_codes", align_bytes=64)
-        v_scales = sb.tile([P, V_BLOCKS, SLOT_PASSES, P], U8, name="v_scales", align_bytes=64)
+        first_got = sb.tile([P, N], BF16, name="first_got", align_bytes=64)
+        nc.scalar.activation(first_got[:], v_bf[:].indirect(offsets[:]), ACT.Copy)
 
-        def values(b):
-            got = sb.tile([P, N], BF16, name=f"v_got{b}", align_bytes=64)
-            nc.vector.tensor_copy(got[:], v_pool[b][:].indirect(offsets[:]))
-            words = got[:].bitcast(F32)
-            bank = ps.tile([P, SLOT_PASSES, 2, P], F32, name=f"v_bank{b}")
+        def turn_values(b, got, v_words):
+            bank = ps.tile([P, SLOT_PASSES, 2, P], F32, name=f"v_bank{b}", tag=f"v_bank{b}")
             for g in range(SLOT_PASSES):
+                words = got[:, g * K_PASS : (g + 1) * K_PASS].bitcast(F32)
                 for u in range(2):
-                    nc.tensor.transpose(bank[:, g, u, :], words[:, 256 * g + u : 256 * (g + 1) : 2], ident[:])
-            v_words = sb.tile([P, SLOT_PASSES, P, 2], F32, name=f"v_words{b}", align_bytes=64)
+                    nc.tensor.transpose(bank[:, g, u, :], words[:, u::2], ident[:])
             nc.scalar.copy(v_words[:], bank[:].rearrange("p g u e -> p g e u"))
-            return v_words
+
+        first_turned = sb.tile([P, SLOT_PASSES, P, 2], F32, name="first_turned", tag="queries", align_bytes=64)
+        turn_values(0, first_got, first_turned)
+        v_codes = shared.tile([P, V_BLOCKS, SLOT_PASSES, P], U32, name="v_codes", offset=2048, align_bytes=64)
+        v_scales = sb.tile([P, V_BLOCKS, SLOT_PASSES, P], U8, name="v_scales", align_bytes=64)
 
         def quantise_values(b, v_words):
             nc.vector.quantize_mx(
@@ -161,14 +133,63 @@ def tile_attend_sigm_cap_srtq256n1024t2048_kernel(tc, qT, k_words, k_scales, vT,
                 in_=v_words[:].rearrange("p g e u -> p (g e u)").bitcast(BF16),
             )
 
-        v_turned = [values(b) for b in range(V_BLOCKS)]
-        w_bf = sb.tile([P, Q_BLOCKS, SLOT_PASSES, P, PACK], BF16, name="w_bf", tag="values1", align_bytes=64)
-        w_codes = sb.tile([P, Q_BLOCKS, SLOT_PASSES, P], U32, name="w_codes", align_bytes=64)
-        w_scales = sb.tile([P, Q_BLOCKS, SLOT_PASSES, P], U8, name="w_scales", align_bytes=64)
+        kw_use = []
+        for g in range(SLOT_PASSES):
+            reach = T - N + (g + 1) * K_PASS
+            if g == 0:
+                kw_got = sb.tile([P, K_PASS], U32, name="kw_got0", align_bytes=64)
+            else:
+                kw_got = shared.tile([P, K_PASS], U32, name="kw_got1", offset=0, align_bytes=64)
+            nc.vector.tensor_copy(
+                kw_got[:], kw_pool[:, :reach].bitcast(U32).indirect(offsets[:, g * 32 : (g + 1) * 32])
+            )
+            parted = sb.tile([P, D_PASSES, K_PASS], U16, name=f"kw_use{g}", align_bytes=64)
+            nc.vector.tensor_copy(parted[:], kw_got[:].bitcast(U16).rearrange("x (n o) -> x o n", o=D_PASSES))
+            kw_use.append(parted)
+        quantise_values(0, first_turned)
+        second_got = sb.tile([P, N], BF16, name="second_got", align_bytes=64)
+        nc.vector.tensor_copy(second_got[:], v_second[:].indirect(offsets[:]))
+
+        turned = {}
+        for g in range(SLOT_PASSES):
+            inner = [sb.tile([P, PACK, P], F32, name=f"inner{g}{h}", tag=f"inner{h}", align_bytes=64) for h in range(Q_BLOCKS)]
+            for h in range(Q_BLOCKS):
+                qs = slice(h * P, (h + 1) * P)
+                bank = ps.tile([P, K_PASS], F32, name=f"score{g}{h}", tag=f"score{g}{h}")
+                for o in range(D_PASSES):
+                    nc.tensor.matmul_mx(
+                        bank[:],
+                        lhsT=q_codes[:, o, qs].bitcast(FP8X4),
+                        lhsT_scale=q_scales[:, o, qs],
+                        rhs=kw_use[g][:, o, :].bitcast(FP4X4),
+                        rhs_scale=ks_bytes[:, o * N + g * K_PASS : o * N + (g + 1) * K_PASS],
+                        start=(o == 0),
+                        stop=(o == D_PASSES - 1),
+                    )
+                nc.scalar.activation(
+                    inner[h][:].rearrange("q t p -> q p t"),
+                    bank[:].rearrange("q (p t) -> q p t", t=PACK),
+                    ACT.Tanh,
+                    bias=zero[:],
+                    scale=0.5,
+                )
+            for h in range(Q_BLOCKS):
+                outer = sb.tile([P, PACK, P], F32, name=f"outer{g}{h}")
+                nc.scalar.activation(outer[:], inner[h][:], ACT.Tanh, bias=zero[:])
+                flip = ps.tile([P, PACK, P], F32, name=f"flip{g}{h}", tag=(f"turn{h}" if g == 0 else f"score0{h}"))
+                for t in range(PACK):
+                    nc.tensor.transpose(flip[:, t, :], outer[:, t, :], ident[:])
+                turned[g, h] = flip
+
+        second_turned = sb.tile([P, SLOT_PASSES, P, 2], F32, name="second_turned", tag="inner0", align_bytes=64)
+        turn_values(1, second_got, second_turned)
+        w_bf = sb.tile([P, SLOT_PASSES, Q_BLOCKS, P, PACK], BF16, name="w_bf", align_bytes=64)
+        w_codes = sb.tile([P, SLOT_PASSES, Q_BLOCKS, P], U32, name="w_codes", align_bytes=64)
+        w_scales = sb.tile([P, SLOT_PASSES, Q_BLOCKS, P], U8, name="w_scales", align_bytes=64)
 
         def weights(g, h):
             nc.vector.scalar_tensor_tensor(
-                w_bf[:, h, g],
+                w_bf[:, g, h],
                 turned[g, h][:].rearrange("p t q -> p q t"),
                 1.0,
                 vs_col[g][:].unsqueeze(1).to_broadcast([P, P, PACK]),
@@ -176,38 +197,40 @@ def tile_attend_sigm_cap_srtq256n1024t2048_kernel(tc, qT, k_words, k_scales, vT,
                 ALU.mult,
             )
 
-        def quantise_weights(g, h):
+        def quantise_weights(g, hs):
             nc.vector.quantize_mx(
-                out=w_codes[:, h, g].bitcast(FP8X4),
-                scales=w_scales[:, h, g],
-                in_=w_bf[:, h, g].rearrange("p q t -> p (q t)"),
+                out=w_codes[:, g, hs].rearrange("p h q -> p (h q)").bitcast(FP8X4),
+                scales=w_scales[:, g, hs].rearrange("p h q -> p (h q)"),
+                in_=w_bf[:, g, hs].rearrange("p h q t -> p (h q t)"),
             )
 
-        quantise_values(0, v_turned[0])
         weights(0, 0)
-        weights(1, 0)
-        quantise_weights(0, 0)
-        quantise_values(1, v_turned[1])
-        quantise_weights(1, 0)
         weights(0, 1)
+        weights(1, 0)
+        quantise_weights(0, slice(0, 2))
         weights(1, 1)
-        quantise_weights(0, 1)
-        quantise_weights(1, 1)
+        quantise_weights(1, slice(0, 1))
+        quantise_values(1, second_turned)
+        quantise_weights(1, slice(1, 2))
 
+        spare = {(0, 0): "score10", (0, 1): "turn0", (1, 0): "score11", (1, 1): "v_bank0"}
         for h in range(Q_BLOCKS):
             qs = slice(h * P, (h + 1) * P)
-            acc = ps.tile([P, V_BLOCKS, P], F32, name=f"acc{h}", tag=f"score{h}1")
+            result = sb.tile([P, V_BLOCKS, P], F32, name=f"result{h}")
             for b in range(V_BLOCKS):
+                acc = ps.tile([P, P], F32, name=f"acc{h}{b}", tag=spare[h, b])
                 for g in range(SLOT_PASSES):
                     nc.tensor.matmul_mx(
-                        acc[:, b, :],
-                        lhsT=w_codes[:, h, g].bitcast(FP8X4),
-                        lhsT_scale=w_scales[:, h, g],
+                        acc[:],
+                        lhsT=w_codes[:, g, h].bitcast(FP8X4),
+                        lhsT_scale=w_scales[:, g, h],
                         rhs=v_codes[:, b, g].bitcast(FP8X4),
                         rhs_scale=v_scales[:, b, g],
                         start=(g == 0),
                         stop=(g == SLOT_PASSES - 1),
                     )
-            result = sb.tile([P, DV], F32, name=f"result{h}")
-            nc.scalar.activation(result[:], acc[:].rearrange("q b e -> q (b e)"), ACT.Copy, scale=1.0 / 32.0)
-            nc.sync.dma_start(out[0, qs, :], result[:])
+                if (h, b) == (1, 1):
+                    nc.vector.tensor_scalar_mul(result[:, b, :], acc[:], 1.0 / 32.0)
+                else:
+                    nc.scalar.activation(result[:, b, :], acc[:], ACT.Copy, scale=1.0 / 32.0)
+            nc.sync.dma_start(out[0, qs, :], result[:].rearrange("q b e -> q (b e)"))

@@ -64,15 +64,14 @@ def tile_attend_sigm_cap_srtq256n1024t2048_kernel(tc, qT, k_words, k_scales, vT,
         nc.scalar.activation(zero[:], zero_in[:], ACT.Tanh)
         nc.vector.memset(ks_pool[0:96, :], 0)
         ks_use = sb.tile([P, D_PASSES, N // 4], I32, name="ks_use", align_bytes=64)
-        nc.gpsimd.memset(ks_use[:], 0)
+        nc.vector.memset(ks_use[:], 0)
 
         kw_pool = sb.tile([P, T], I32, name="kw_pool", align_bytes=64)
         kw_dram = k_words[0].rearrange("p t b -> p (t b)").bitcast(I32)
         q_raw = sb.tile([P, D_PASSES, PACK, NQ], F32, name="q_raw", tag="queries", align_bytes=64)
         nc.sync.dma_start(kw_pool[:, :1536], kw_dram[:, :1536])
-        for o in range(D_PASSES):
-            nc.sync.dma_start(q_raw[:, o], qT[0, o * K_PASS : (o + 1) * K_PASS, :].rearrange("(p j) q -> p j q", j=PACK))
-        nc.sync.dma_start(kw_pool[:, 1536:], kw_dram[:, 1536:])
+        q_dram = qT[0].rearrange("(o p j) q -> o p j q", o=D_PASSES, j=PACK)
+        nc.sync.dma_start(q_raw[:, 0], q_dram[0])
 
         ks_got = sb.tile([P, N], U8, name="ks_got", align_bytes=64)
         nc.vector.tensor_copy(ks_got[:], ks_pool[:].bitcast(U8).indirect(offsets[:]))
@@ -83,6 +82,8 @@ def tile_attend_sigm_cap_srtq256n1024t2048_kernel(tc, qT, k_words, k_scales, vT,
             )
         ks_bytes = ks_use[:].rearrange("x o n -> x (o n)").bitcast(U8)
 
+        nc.sync.dma_start(q_raw[:, 1], q_dram[1])
+        nc.sync.dma_start(kw_pool[:, 1536:], kw_dram[:, 1536:])
         v_second = sb.tile([P, T], F32, name="v_second", align_bytes=64)
         nc.sync.dma_start(v_second[:], vT[P : 2 * P, :])
 
@@ -101,8 +102,8 @@ def tile_attend_sigm_cap_srtq256n1024t2048_kernel(tc, qT, k_words, k_scales, vT,
         q_bf = shared.tile([P, D_PASSES, NQ, PACK], BF16, name="q_bf", offset=0, align_bytes=64)
         woven = [q_bf[:, o].rearrange("p (c i) j -> p c j i", i=PACK) for o in range(D_PASSES)]
         rows = [q_raw[:, o].rearrange("p j (c i) -> p c j i", i=PACK) for o in range(D_PASSES)]
-        nc.scalar.copy(woven[0], rows[0])
-        nc.vector.tensor_copy(woven[1], rows[1])
+        nc.vector.tensor_copy(woven[0], rows[0])
+        nc.scalar.copy(woven[1], rows[1])
         for o in range(D_PASSES):
             nc.vector.quantize_mx(
                 out=q_codes[:, o].bitcast(FP8X4),

@@ -102,9 +102,8 @@ def tile_attend_sigm_cap_srtq256n1024t2048_kernel(tc, qT, k_words, k_scales, vT,
         q_bf = shared.tile([P, D_PASSES, NQ, PACK], BF16, name="q_bf", offset=0, align_bytes=64)
         woven = [q_bf[:, o].rearrange("p (c i) j -> p c j i", i=PACK) for o in range(D_PASSES)]
         rows = [q_raw[:, o].rearrange("p j (c i) -> p c j i", i=PACK) for o in range(D_PASSES)]
-        nc.vector.tensor_copy(woven[0], rows[0])
-        nc.scalar.copy(woven[1], rows[1])
         for o in range(D_PASSES):
+            nc.vector.tensor_copy(woven[o], rows[o])
             nc.vector.quantize_mx(
                 out=q_codes[:, o].bitcast(FP8X4),
                 scales=q_scales[:, o],

@@ -69,9 +69,10 @@ def tile_attend_sigm_cap_srtq256n1024t2048_kernel(tc, qT, k_words, k_scales, vT,
         kw_pool = sb.tile([P, T], I32, name="kw_pool", align_bytes=64)
         kw_dram = k_words[0].rearrange("p t b -> p (t b)").bitcast(I32)
         q_raw = sb.tile([P, D_PASSES, PACK, NQ], F32, name="q_raw", tag="queries", align_bytes=64)
-        nc.sync.dma_start(kw_pool[:, :1536], kw_dram[:, :1536])
+        nc.sync.dma_start(kw_pool[:, :1024], kw_dram[:, :1024])
         q_dram = qT[0].rearrange("(o p j) q -> o p j q", o=D_PASSES, j=PACK)
         nc.sync.dma_start(q_raw[:, 0], q_dram[0])
+        nc.sync.dma_start(kw_pool[:, 1024:1536], kw_dram[:, 1024:1536])
 
         ks_got = sb.tile([P, N], U8, name="ks_got", align_bytes=64)
         nc.vector.tensor_copy(ks_got[:], ks_pool[:].bitcast(U8).indirect(offsets[:]))
@@ -102,8 +103,11 @@ def tile_attend_sigm_cap_srtq256n1024t2048_kernel(tc, qT, k_words, k_scales, vT,
         q_bf = shared.tile([P, D_PASSES, NQ, PACK], BF16, name="q_bf", offset=0, align_bytes=64)
         woven = [q_bf[:, o].rearrange("p (c i) j -> p c j i", i=PACK) for o in range(D_PASSES)]
         rows = [q_raw[:, o].rearrange("p j (c i) -> p c j i", i=PACK) for o in range(D_PASSES)]
+        half = NQ // PACK // 2
+        nc.vector.tensor_copy(woven[0], rows[0])
+        nc.vector.tensor_copy(woven[1][:, :half], rows[1][:, :half])
+        nc.scalar.copy(woven[1][:, half:], rows[1][:, half:])
         for o in range(D_PASSES):
-            nc.vector.tensor_copy(woven[o], rows[o])
             nc.vector.quantize_mx(
                 out=q_codes[:, o].bitcast(FP8X4),
                 scales=q_scales[:, o],

@@ -43,8 +43,7 @@ def tile_attend_sigm_cap_srtq256n1024t2048_kernel(tc, qT, k_words, k_scales, vT,
             nc.sync.dma_start(v_first[:, cols], vT[0:P, cols])
 
         vs_pool = sb.tile([P, T], F32, name="vs_pool", align_bytes=64)
-        nc.gpsimd.memset(vs_pool[:, halves[0]], 0.0)
-        nc.vector.memset(vs_pool[:, halves[1]], 0.0)
+        nc.vector.memset(vs_pool[:], 0.0)
         nc.sync.dma_start(vs_pool[0:1, :], vs[0:1, :])
         blank = sb.tile([P, P], F32, name="blank")
         nc.gpsimd.memset(blank[:], 0.0)

@@ -170,8 +170,8 @@ def tile_attend_sigm_cap_srtq256n1024t2048_kernel(tc, qT, k_words, k_scales, vT,
                         stop=(o == D_PASSES - 1),
                     )
                 nc.scalar.activation(
-                    inner[h][:].rearrange("q t p -> q p t"),
-                    bank[:].rearrange("q (p t) -> q p t", t=PACK),
+                    inner[h][:].rearrange("q t (c i) -> q c t i", i=PACK),
+                    bank[:].rearrange("q (c i t) -> q c t i", i=PACK, t=PACK),
                     ACT.Tanh,
                     bias=zero[:],
                     scale=0.5,

@@ -33,10 +33,9 @@ def tile_attend_sigm_cap_srtq256n1024t2048_kernel(tc, qT, k_words, k_scales, vT,
         ps = ctx.enter_context(tc.psum_pool(name="ps", bufs=1))
 
         offsets = sb.tile([P, N // 16], U16, name="offsets")
-        nc.sync.dma_start(offsets[:], offs)
-
         ks_pool = sb.tile([P, T // 4], I32, name="ks_pool", align_bytes=64)
         nc.sync.dma_start(ks_pool[96:128, :], k_scales.rearrange("o f t -> f o t").bitcast(I32))
+        nc.sync.dma_start(offsets[:], offs)
         v_first = sb.tile([P, T], F32, name="v_first", align_bytes=64)
         halves = [slice(0, T // 2), slice(T // 2, T)]
         for cols in halves:
@@ -45,7 +44,13 @@ def tile_attend_sigm_cap_srtq256n1024t2048_kernel(tc, qT, k_words, k_scales, vT,
         vs_pool = sb.tile([P, T], F32, name="vs_pool", align_bytes=64)
         nc.vector.memset(vs_pool[:], 0.0)
         nc.sync.dma_start(vs_pool[0:1, :], vs[0:1, :])
-        blank = sb.tile([P, P], F32, name="blank")
+        zero_in = shared.tile([P, 32], F32, name="zero_in", offset=10176, align_bytes=64)
+        nc.vector.memset(zero_in[:], 0.0)
+        zero = sb.tile([P, 1], F32, name="zero")
+        nc.scalar.activation(zero[:], zero_in[:, 0:1], ACT.Tanh)
+        ks_use = shared.tile([P, D_PASSES, N // 4], I32, name="ks_use", offset=8192, align_bytes=64)
+        nc.gpsimd.memset(ks_use[:], 0)
+        blank = shared.tile([P, P], F32, name="blank", offset=10240, align_bytes=64)
         nc.gpsimd.memset(blank[:], 0.0)
         ident = sb.tile([P, P], F32, name="ident")
         nc.gpsimd.affine_select(
@@ -57,13 +62,7 @@ def tile_attend_sigm_cap_srtq256n1024t2048_kernel(tc, qT, k_words, k_scales, vT,
             pattern=[[-1, P]],
             channel_multiplier=1,
         )
-        zero_in = sb.tile([P, 1], F32, name="zero_in")
-        nc.vector.memset(zero_in[:], 0.0)
-        zero = sb.tile([P, 1], F32, name="zero")
-        nc.scalar.activation(zero[:], zero_in[:], ACT.Tanh)
         nc.vector.memset(ks_pool[0:96, :], 0)
-        ks_use = sb.tile([P, D_PASSES, N // 4], I32, name="ks_use", align_bytes=64)
-        nc.vector.memset(ks_use[:], 0)
 
         kw_pool = sb.tile([P, T], I32, name="kw_pool", align_bytes=64)
         kw_dram = k_words[0].rearrange("p t b -> p (t b)").bitcast(I32)

@@ -128,11 +128,11 @@ def tile_attend_sigm_cap_srtq256n1024t2048_kernel(tc, qT, k_words, k_scales, vT,
         v_codes = shared.tile([P, V_BLOCKS, SLOT_PASSES, P], U32, name="v_codes", offset=2048, align_bytes=64)
         v_scales = sb.tile([P, V_BLOCKS, SLOT_PASSES, P], U8, name="v_scales", align_bytes=64)
 
-        def quantise_values(b, v_words):
+        def quantise_values(b, v_words, gs):
             nc.vector.quantize_mx(
-                out=v_codes[:, b].rearrange("p g e -> p (g e)").bitcast(FP8X4),
-                scales=v_scales[:, b].rearrange("p g e -> p (g e)"),
-                in_=v_words[:].rearrange("p g e u -> p (g e u)").bitcast(BF16),
+                out=v_codes[:, b, gs].rearrange("p g e -> p (g e)").bitcast(FP8X4),
+                scales=v_scales[:, b, gs].rearrange("p g e -> p (g e)"),
+                in_=v_words[:, gs].rearrange("p g e u -> p (g e u)").bitcast(BF16),
             )
 
         kw_use = []
@@ -148,7 +148,7 @@ def tile_attend_sigm_cap_srtq256n1024t2048_kernel(tc, qT, k_words, k_scales, vT,
             parted = sb.tile([P, D_PASSES, K_PASS], U16, name=f"kw_use{g}", align_bytes=64)
             nc.vector.tensor_copy(parted[:], kw_got[:].bitcast(U16).rearrange("x (n o) -> x o n", o=D_PASSES))
             kw_use.append(parted)
-        quantise_values(0, first_turned)
+        quantise_values(0, first_turned, slice(0, 2))
         second_got = sb.tile([P, N], BF16, name="second_got", align_bytes=64)
         nc.vector.tensor_copy(second_got[:], v_second[:].indirect(offsets[:]))
 
@@ -210,20 +210,21 @@ def tile_attend_sigm_cap_srtq256n1024t2048_kernel(tc, qT, k_words, k_scales, vT,
         weights(0, 1)
         weights(1, 0)
         quantise_weights(0, slice(0, 2))
-        weights(1, 1)
+        quantise_values(1, second_turned, slice(0, 1))
         quantise_weights(1, slice(0, 1))
-        quantise_values(1, second_turned)
+        weights(1, 1)
+        quantise_values(1, second_turned, slice(1, 2))
         quantise_weights(1, slice(1, 2))
 
         spare = {(0, 0): "score10", (0, 1): "turn0", (1, 0): "score11", (1, 1): "v_bank0"}
         for h in range(Q_BLOCKS):
             qs = slice(h * P, (h + 1) * P)
             result = sb.tile([P, V_BLOCKS, P], F32, name=f"result{h}")
-            for b in range(V_BLOCKS):
-                acc = ps.tile([P, P], F32, name=f"acc{h}{b}", tag=spare[h, b])
-                for g in range(SLOT_PASSES):
+            accs = [ps.tile([P, P], F32, name=f"acc{h}{b}", tag=spare[h, b]) for b in range(V_BLOCKS)]
+            for g in range(SLOT_PASSES):
+                for b in range(V_BLOCKS):
                     nc.tensor.matmul_mx(
-                        acc[:],
+                        accs[b][:],
                         lhsT=w_codes[:, g, h].bitcast(FP8X4),
                         lhsT_scale=w_scales[:, g, h],
                         rhs=v_codes[:, b, g].bitcast(FP8X4),
@@ -231,6 +232,8 @@ def tile_attend_sigm_cap_srtq256n1024t2048_kernel(tc, qT, k_words, k_scales, vT,
                         start=(g == 0),
                         stop=(g == SLOT_PASSES - 1),
                     )
+            for b in range(V_BLOCKS):
+                acc = accs[b]
                 if (h, b) == (1, 1):
                     nc.vector.tensor_scalar_mul(result[:, b, :], acc[:], 1.0 / 32.0)
                 else:

@@ -32,25 +32,32 @@ def tile_attend_sigm_cap_srtq256n1024t2048_kernel(tc, qT, k_words, k_scales, vT,
         shared = ctx.enter_context(tc.tile_pool(name="shared", bufs=1))
         ps = ctx.enter_context(tc.psum_pool(name="ps", bufs=1))
 
+        def bank_tile(number, shape, name):
+            return ps.tile(shape, F32, name=name, offset=2048 * number)
+
         offsets = sb.tile([P, N // 16], U16, name="offsets")
         ks_pool = sb.tile([P, T // 4], I32, name="ks_pool", align_bytes=64)
         nc.sync.dma_start(ks_pool[96:128, :], k_scales.rearrange("o f t -> f o t").bitcast(I32))
         nc.sync.dma_start(offsets[:], offs)
+        q_dram = qT[0].rearrange("(o p j) q -> o p j q", o=D_PASSES, j=PACK)
+        q_raw = sb.tile([P, D_PASSES, PACK, NQ], F32, name="q_raw", tag="queries", align_bytes=64)
         v_first = sb.tile([P, T], F32, name="v_first", align_bytes=64)
         halves = [slice(0, T // 2), slice(T // 2, T)]
         for cols in halves:
             nc.sync.dma_start(v_first[:, cols], vT[0:P, cols])
-
+        nc.gpsimd.memset(ks_pool[0:96, :], 0)
         vs_pool = sb.tile([P, T], F32, name="vs_pool", align_bytes=64)
-        nc.vector.memset(vs_pool[:], 0.0)
+        nc.gpsimd.memset(vs_pool[:, :1024], 0.0)
+        nc.vector.memset(vs_pool[:, 1024:1535], 0.0)
+        nc.vector.memset(vs_pool[:, 1535:], 0.0)
         nc.sync.dma_start(vs_pool[0:1, :], vs[0:1, :])
-        zero_in = shared.tile([P, 32], F32, name="zero_in", offset=10176, align_bytes=64)
-        nc.vector.memset(zero_in[:], 0.0)
         zero = sb.tile([P, 1], F32, name="zero")
-        nc.scalar.activation(zero[:], zero_in[:, 0:1], ACT.Tanh)
-        ks_use = shared.tile([P, D_PASSES, N // 4], I32, name="ks_use", offset=8192, align_bytes=64)
+        nc.vector.memset(zero[:], 0.0)
+        half_scale = sb.tile([P, 1], F32, name="half_scale")
+        nc.scalar.activation(half_scale[:], zero[:], ACT.Sigmoid, bias=zero[:])
+        ks_use = sb.tile([P, D_PASSES, N // 4], I32, name="ks_use", align_bytes=64)
         nc.gpsimd.memset(ks_use[:], 0)
-        blank = shared.tile([P, P], F32, name="blank", offset=10240, align_bytes=64)
+        blank = sb.tile([P, P], F32, name="blank", align_bytes=64)
         nc.gpsimd.memset(blank[:], 0.0)
         ident = sb.tile([P, P], F32, name="ident")
         nc.gpsimd.affine_select(
@@ -62,13 +69,10 @@ def tile_attend_sigm_cap_srtq256n1024t2048_kernel(tc, qT, k_words, k_scales, vT,
             pattern=[[-1, P]],
             channel_multiplier=1,
         )
-        nc.vector.memset(ks_pool[0:96, :], 0)
 
         kw_pool = sb.tile([P, T], I32, name="kw_pool", align_bytes=64)
         kw_dram = k_words[0].rearrange("p t b -> p (t b)").bitcast(I32)
-        q_raw = sb.tile([P, D_PASSES, PACK, NQ], F32, name="q_raw", tag="queries", align_bytes=64)
         nc.sync.dma_start(kw_pool[:, :1024], kw_dram[:, :1024])
-        q_dram = qT[0].rearrange("(o p j) q -> o p j q", o=D_PASSES, j=PACK)
         nc.sync.dma_start(q_raw[:, 0], q_dram[0])
         nc.sync.dma_start(kw_pool[:, 1024:1536], kw_dram[:, 1024:1536])
 
@@ -92,16 +96,16 @@ def tile_attend_sigm_cap_srtq256n1024t2048_kernel(tc, qT, k_words, k_scales, vT,
         for g in range(SLOT_PASSES):
             nc.sync.dma_start(vs_col[g][:], vs_got[0:1, g * K_PASS : (g + 1) * K_PASS])
 
-        v_bf = sb.tile([P, T], BF16, name="v_bf", align_bytes=64)
-        for cols in halves:
-            nc.scalar.activation(v_bf[:, cols], v_first[:, cols], ACT.Copy)
-
         q_codes = sb.tile([P, D_PASSES, NQ], U32, name="q_codes", align_bytes=64)
         q_scales = sb.tile([P, D_PASSES, NQ], U8, name="q_scales", align_bytes=64)
         q_bf = shared.tile([P, D_PASSES, NQ, PACK], BF16, name="q_bf", offset=0, align_bytes=64)
         woven = [q_bf[:, o].rearrange("p (c i) j -> p c j i", i=PACK) for o in range(D_PASSES)]
         rows = [q_raw[:, o].rearrange("p j (c i) -> p c j i", i=PACK) for o in range(D_PASSES)]
         half = NQ // PACK // 2
+
+        v_bf = sb.tile([P, T], BF16, name="v_bf", align_bytes=64)
+        for cols in halves:
+            nc.scalar.activation(v_bf[:, cols], v_first[:, cols], ACT.Copy)
         nc.vector.tensor_copy(woven[0], rows[0])
         nc.vector.tensor_copy(woven[1][:, :half], rows[1][:, :half])
         nc.scalar.copy(woven[1][:, half:], rows[1][:, half:])
@@ -115,8 +119,8 @@ def tile_attend_sigm_cap_srtq256n1024t2048_kernel(tc, qT, k_words, k_scales, vT,
         first_got = sb.tile([P, N], BF16, name="first_got", align_bytes=64)
         nc.scalar.activation(first_got[:], v_bf[:].indirect(offsets[:]), ACT.Copy)
 
-        def turn_values(b, got, v_words):
-            bank = ps.tile([P, SLOT_PASSES, 2, P], F32, name=f"v_bank{b}", tag=f"v_bank{b}")
+        def turn_values(b, got, v_words, number):
+            bank = bank_tile(number, [P, SLOT_PASSES, 2, P], f"v_bank{b}")
             for g in range(SLOT_PASSES):
                 words = got[:, g * K_PASS : (g + 1) * K_PASS].bitcast(F32)
                 for u in range(2):
@@ -124,7 +128,7 @@ def tile_attend_sigm_cap_srtq256n1024t2048_kernel(tc, qT, k_words, k_scales, vT,
             nc.scalar.copy(v_words[:], bank[:].rearrange("p g u e -> p g e u"))
 
         first_turned = sb.tile([P, SLOT_PASSES, P, 2], F32, name="first_turned", tag="queries", align_bytes=64)
-        turn_values(0, first_got, first_turned)
+        turn_values(0, first_got, first_turned, 6)
         v_codes = shared.tile([P, V_BLOCKS, SLOT_PASSES, P], U32, name="v_codes", offset=2048, align_bytes=64)
         v_scales = sb.tile([P, V_BLOCKS, SLOT_PASSES, P], U8, name="v_scales", align_bytes=64)
 
@@ -152,12 +156,12 @@ def tile_attend_sigm_cap_srtq256n1024t2048_kernel(tc, qT, k_words, k_scales, vT,
         second_got = sb.tile([P, N], BF16, name="second_got", align_bytes=64)
         nc.vector.tensor_copy(second_got[:], v_second[:].indirect(offsets[:]))
 
-        turned = {}
+        gate = {}
         for g in range(SLOT_PASSES):
-            inner = [sb.tile([P, PACK, P], F32, name=f"inner{g}{h}", tag=f"inner{h}", align_bytes=64) for h in range(Q_BLOCKS)]
+            inner, flip = [], []
             for h in range(Q_BLOCKS):
                 qs = slice(h * P, (h + 1) * P)
-                bank = ps.tile([P, K_PASS], F32, name=f"score{g}{h}", tag=f"score{g}{h}")
+                bank = bank_tile(2 * g + h, [P, K_PASS], f"score{g}{h}")
                 for o in range(D_PASSES):
                     nc.tensor.matmul_mx(
                         bank[:],
@@ -168,61 +172,71 @@ def tile_attend_sigm_cap_srtq256n1024t2048_kernel(tc, qT, k_words, k_scales, vT,
                         start=(o == 0),
                         stop=(o == D_PASSES - 1),
                     )
+                inner.append(shared.tile([P, PACK, P], F32, name=f"inner{g}{h}", offset=4096 + 2048 * h, align_bytes=64))
                 nc.scalar.activation(
                     inner[h][:].rearrange("q t (c i) -> q c t i", i=PACK),
                     bank[:].rearrange("q (c i t) -> q c t i", i=PACK, t=PACK),
                     ACT.Tanh,
                     bias=zero[:],
-                    scale=0.5,
+                    scale=half_scale[:],
                 )
-            for h in range(Q_BLOCKS):
-                outer = sb.tile([P, PACK, P], F32, name=f"outer{g}{h}")
-                nc.scalar.activation(outer[:], inner[h][:], ACT.Tanh, bias=zero[:])
-                flip = ps.tile([P, PACK, P], F32, name=f"flip{g}{h}", tag=(f"turn{h}" if g == 0 else f"score0{h}"))
-                for t in range(PACK):
-                    nc.tensor.transpose(flip[:, t, :], outer[:, t, :], ident[:])
-                turned[g, h] = flip
+                flip.append(bank_tile(4 * (1 - g) + h, [P, PACK, P], f"flip{g}{h}"))
+            if g == 0:
+                for h in range(Q_BLOCKS):
+                    outer = sb.tile([P, PACK, P], F32, name=f"outer{h}", align_bytes=64)
+                    nc.scalar.activation(outer[:], inner[h][:], ACT.Sigmoid, bias=zero[:], scale=2.0)
+                    for t in range(PACK):
+                        nc.tensor.transpose(flip[h][:, t, :], outer[:, t, :], ident[:])
+                    gate[g, h] = flip[h][:].rearrange("p t q -> p q t")
+            else:
+                for h in range(Q_BLOCKS):
+                    for t in range(PACK):
+                        nc.tensor.transpose(flip[h][:, t, :], inner[h][:, t, :], ident[:])
+                for h in range(Q_BLOCKS):
+                    outer = sb.tile([P, P, PACK], F32, name=f"gate{h}", align_bytes=64)
+                    nc.scalar.activation(
+                        outer[:], flip[h][:].rearrange("p t q -> p q t"), ACT.Sigmoid, bias=zero[:], scale=2.0
+                    )
+                    gate[g, h] = outer[:]
 
-        second_turned = sb.tile([P, SLOT_PASSES, P, 2], F32, name="second_turned", tag="inner0", align_bytes=64)
-        turn_values(1, second_got, second_turned)
+        second_turned = shared.tile([P, SLOT_PASSES, P, 2], F32, name="second_turned", offset=6144, align_bytes=64)
+        turn_values(1, second_got, second_turned, 3)
         w_bf = sb.tile([P, SLOT_PASSES, Q_BLOCKS, P, PACK], BF16, name="w_bf", align_bytes=64)
         w_codes = sb.tile([P, SLOT_PASSES, Q_BLOCKS, P], U32, name="w_codes", align_bytes=64)
         w_scales = sb.tile([P, SLOT_PASSES, Q_BLOCKS, P], U8, name="w_scales", align_bytes=64)
 
         def weights(g, h):
-            nc.vector.scalar_tensor_tensor(
+            nc.vector.tensor_tensor(
                 w_bf[:, g, h],
-                turned[g, h][:].rearrange("p t q -> p q t"),
-                1.0,
+                gate[g, h],
                 vs_col[g][:].unsqueeze(1).to_broadcast([P, P, PACK]),
-                ALU.add,
                 ALU.mult,
             )
 
-        def quantise_weights(g, hs):
+        def quantise_weights(g, h):
             nc.vector.quantize_mx(
-                out=w_codes[:, g, hs].rearrange("p h q -> p (h q)").bitcast(FP8X4),
-                scales=w_scales[:, g, hs].rearrange("p h q -> p (h q)"),
-                in_=w_bf[:, g, hs].rearrange("p h q t -> p (h q t)"),
+                out=w_codes[:, g, h].bitcast(FP8X4),
+                scales=w_scales[:, g, h],
+                in_=w_bf[:, g, h].rearrange("p q t -> p (q t)"),
             )
 
         weights(0, 0)
         weights(0, 1)
+        quantise_weights(0, 0)
         weights(1, 0)
-        quantise_weights(0, slice(0, 2))
-        quantise_values(1, second_turned, slice(0, 1))
-        quantise_weights(1, slice(0, 1))
+        quantise_weights(0, 1)
         weights(1, 1)
-        quantise_values(1, second_turned, slice(1, 2))
-        quantise_weights(1, slice(1, 2))
+        quantise_weights(1, 0)
+        quantise_values(1, second_turned, slice(0, 2))
+        quantise_weights(1, 1)
 
-        spare = {(0, 0): "score10", (0, 1): "turn0", (1, 0): "score11", (1, 1): "v_bank0"}
+        acc_bank = {(0, 0): 2, (0, 1): 6, (1, 0): 7, (1, 1): 4}
         for h in range(Q_BLOCKS):
             qs = slice(h * P, (h + 1) * P)
             result = sb.tile([P, V_BLOCKS, P], F32, name=f"result{h}")
-            accs = [ps.tile([P, P], F32, name=f"acc{h}{b}", tag=spare[h, b]) for b in range(V_BLOCKS)]
-            for g in range(SLOT_PASSES):
-                for b in range(V_BLOCKS):
+            accs = [bank_tile(acc_bank[h, b], [P, P], f"acc{h}{b}") for b in range(V_BLOCKS)]
+            for b in range(V_BLOCKS):
+                for g in range(SLOT_PASSES):
                     nc.tensor.matmul_mx(
                         accs[b][:],
                         lhsT=w_codes[:, g, h].bitcast(FP8X4),
@@ -235,7 +249,7 @@ def tile_attend_sigm_cap_srtq256n1024t2048_kernel(tc, qT, k_words, k_scales, vT,
             for b in range(V_BLOCKS):
                 acc = accs[b]
                 if (h, b) == (1, 1):
-                    nc.vector.tensor_scalar_mul(result[:, b, :], acc[:], 1.0 / 32.0)
+                    nc.vector.tensor_scalar_mul(result[:, b, :], acc[:], 1.0 / 16.0)
                 else:
-                    nc.scalar.activation(result[:, b, :], acc[:], ACT.Copy, scale=1.0 / 32.0)
+                    nc.scalar.activation(result[:, b, :], acc[:], ACT.Copy, scale=1.0 / 16.0)
             nc.sync.dma_start(out[0, qs, :], result[:].rearrange("q b e -> q (b e)"))

@@ -40,10 +40,10 @@ def tile_attend_sigm_cap_srtq256n1024t2048_kernel(tc, qT, k_words, k_scales, vT,
         nc.sync.dma_start(ks_pool[96:128, :], k_scales.rearrange("o f t -> f o t").bitcast(I32))
         nc.sync.dma_start(offsets[:], offs)
         q_dram = qT[0].rearrange("(o p j) q -> o p j q", o=D_PASSES, j=PACK)
-        q_raw = sb.tile([P, D_PASSES, PACK, NQ], F32, name="q_raw", tag="queries", align_bytes=64)
+        q_raw = [sb.tile([P, PACK, NQ], F32, name=f"q_raw{o}", tag=f"queries{o}", align_bytes=64) for o in range(D_PASSES)]
         v_first = sb.tile([P, T], F32, name="v_first", align_bytes=64)
-        halves = [slice(0, T // 2), slice(T // 2, T)]
-        for cols in halves:
+        pieces = [slice(0, 1024), slice(1024, 1536), slice(1536, T)]
+        for cols in pieces[:2]:
             nc.sync.dma_start(v_first[:, cols], vT[0:P, cols])
         nc.gpsimd.memset(ks_pool[0:96, :], 0)
         vs_pool = sb.tile([P, T], F32, name="vs_pool", align_bytes=64)
@@ -72,9 +72,10 @@ def tile_attend_sigm_cap_srtq256n1024t2048_kernel(tc, qT, k_words, k_scales, vT,
 
         kw_pool = sb.tile([P, T], I32, name="kw_pool", align_bytes=64)
         kw_dram = k_words[0].rearrange("p t b -> p (t b)").bitcast(I32)
-        nc.sync.dma_start(kw_pool[:, :1024], kw_dram[:, :1024])
-        nc.sync.dma_start(q_raw[:, 0], q_dram[0])
-        nc.sync.dma_start(kw_pool[:, 1024:1536], kw_dram[:, 1024:1536])
+        nc.sync.dma_start(kw_pool[:, :1536], kw_dram[:, :1536])
+        nc.sync.dma_start(q_raw[0][:], q_dram[0])
+        nc.sync.dma_start(q_raw[1][:], q_dram[1])
+        nc.sync.dma_start(v_first[:, pieces[2]], vT[0:P, pieces[2]])
 
         ks_got = sb.tile([P, N], U8, name="ks_got", align_bytes=64)
         nc.vector.tensor_copy(ks_got[:], ks_pool[:].bitcast(U8).indirect(offsets[:]))
@@ -85,7 +86,6 @@ def tile_attend_sigm_cap_srtq256n1024t2048_kernel(tc, qT, k_words, k_scales, vT,
             )
         ks_bytes = ks_use[:].rearrange("x o n -> x (o n)").bitcast(U8)
 
-        nc.sync.dma_start(q_raw[:, 1], q_dram[1])
         nc.sync.dma_start(kw_pool[:, 1536:], kw_dram[:, 1536:])
         v_second = sb.tile([P, T], F32, name="v_second", align_bytes=64)
         nc.sync.dma_start(v_second[:], vT[P : 2 * P, :])
@@ -98,15 +98,21 @@ def tile_attend_sigm_cap_srtq256n1024t2048_kernel(tc, qT, k_words, k_scales, vT,
 
         q_codes = sb.tile([P, D_PASSES, NQ], U32, name="q_codes", align_bytes=64)
         q_scales = sb.tile([P, D_PASSES, NQ], U8, name="q_scales", align_bytes=64)
-        q_bf = shared.tile([P, D_PASSES, NQ, PACK], BF16, name="q_bf", offset=0, align_bytes=64)
+        q_bf = sb.tile([P, D_PASSES, NQ, PACK], BF16, name="q_bf", align_bytes=64)
         woven = [q_bf[:, o].rearrange("p (c i) j -> p c j i", i=PACK) for o in range(D_PASSES)]
-        rows = [q_raw[:, o].rearrange("p j (c i) -> p c j i", i=PACK) for o in range(D_PASSES)]
+        rows = [q_raw[o][:].rearrange("p j (c i) -> p c j i", i=PACK) for o in range(D_PASSES)]
         half = NQ // PACK // 2
 
         v_bf = sb.tile([P, T], BF16, name="v_bf", align_bytes=64)
-        for cols in halves:
+        for cols in pieces[:2]:
             nc.scalar.activation(v_bf[:, cols], v_first[:, cols], ACT.Copy)
-        nc.vector.tensor_copy(woven[0], rows[0])
+        first_got = [sb.tile([P, K_PASS], BF16, name=f"first_got{g}", align_bytes=64) for g in range(SLOT_PASSES)]
+        nc.scalar.activation(
+            first_got[0][:].rearrange("p (u s e) -> p s u e", u=2, e=2),
+            v_bf[:, :1536].indirect(offsets[:, 0:32]),
+            ACT.Copy,
+        )
+        nc.scalar.copy(woven[0], rows[0])
         nc.vector.tensor_copy(woven[1][:, :half], rows[1][:, :half])
         nc.scalar.copy(woven[1][:, half:], rows[1][:, half:])
         for o in range(D_PASSES):
@@ -116,62 +122,71 @@ def tile_attend_sigm_cap_srtq256n1024t2048_kernel(tc, qT, k_words, k_scales, vT,
                 in_=q_bf[:, o].rearrange("p q j -> p (q j)"),
             )
 
-        first_got = sb.tile([P, N], BF16, name="first_got", align_bytes=64)
-        nc.scalar.activation(first_got[:], v_bf[:].indirect(offsets[:]), ACT.Copy)
+        def turn_pass(bank, got):
+            words = got.bitcast(F32)
+            for u in range(2):
+                nc.tensor.transpose(bank[:, u, :], words[:, u::2], ident[:])
 
-        def turn_values(b, got, v_words, number):
-            bank = bank_tile(number, [P, SLOT_PASSES, 2, P], f"v_bank{b}")
-            for g in range(SLOT_PASSES):
-                words = got[:, g * K_PASS : (g + 1) * K_PASS].bitcast(F32)
-                for u in range(2):
-                    nc.tensor.transpose(bank[:, g, u, :], words[:, u::2], ident[:])
-            nc.scalar.copy(v_words[:], bank[:].rearrange("p g u e -> p g e u"))
+        early_bank = bank_tile(6, [P, 2, P], "early_bank")
+        for u in range(2):
+            nc.tensor.transpose(early_bank[:, u, :], first_got[0][:].bitcast(F32)[:, u * P : (u + 1) * P], ident[:])
+        early_words = sb.tile([P, 1, P, 2], F32, name="early_words", tag="queries0", align_bytes=64)
+        nc.scalar.copy(early_words[:, 0], early_bank[:].rearrange("p u e -> p e u"))
+        nc.scalar.activation(v_bf[:, pieces[2]], v_first[:, pieces[2]], ACT.Copy)
+        nc.scalar.activation(first_got[1][:], v_bf[:].indirect(offsets[:, 32:64]), ACT.Copy)
+        v_codes = sb.tile([P, V_BLOCKS * SLOT_PASSES * P], U32, name="v_codes", align_bytes=64)
+        v_scales = sb.tile([P, V_BLOCKS * SLOT_PASSES * P], U8, name="v_scales", align_bytes=64)
 
-        first_turned = sb.tile([P, SLOT_PASSES, P, 2], F32, name="first_turned", tag="queries", align_bytes=64)
-        turn_values(0, first_got, first_turned, 6)
-        v_codes = shared.tile([P, V_BLOCKS, SLOT_PASSES, P], U32, name="v_codes", offset=2048, align_bytes=64)
-        v_scales = sb.tile([P, V_BLOCKS, SLOT_PASSES, P], U8, name="v_scales", align_bytes=64)
-
-        def quantise_values(b, v_words, gs):
+        def quantise_values(first, v_words):
+            cols = slice(first * P, (first + v_words.shape[1]) * P)
             nc.vector.quantize_mx(
-                out=v_codes[:, b, gs].rearrange("p g e -> p (g e)").bitcast(FP8X4),
-                scales=v_scales[:, b, gs].rearrange("p g e -> p (g e)"),
-                in_=v_words[:, gs].rearrange("p g e u -> p (g e u)").bitcast(BF16),
+                out=v_codes[:, cols].bitcast(FP8X4),
+                scales=v_scales[:, cols],
+                in_=v_words.rearrange("p g e u -> p (g e u)").bitcast(BF16),
             )
+
+        quantise_values(0, early_words[:])
 
         kw_use = []
         for g in range(SLOT_PASSES):
             reach = T - N + (g + 1) * K_PASS
-            if g == 0:
-                kw_got = sb.tile([P, K_PASS], U32, name="kw_got0", align_bytes=64)
-            else:
-                kw_got = shared.tile([P, K_PASS], U32, name="kw_got1", offset=0, align_bytes=64)
-            nc.vector.tensor_copy(
-                kw_got[:], kw_pool[:, :reach].bitcast(U32).indirect(offsets[:, g * 32 : (g + 1) * 32])
-            )
             parted = sb.tile([P, D_PASSES, K_PASS], U16, name=f"kw_use{g}", align_bytes=64)
-            nc.vector.tensor_copy(parted[:], kw_got[:].bitcast(U16).rearrange("x (n o) -> x o n", o=D_PASSES))
+            kw_got = [sb.tile([P, 256], U32, name=f"kw_got{g}{j}", align_bytes=64) for j in range(2)]
+            for j in range(2):
+                first = g * 32 + j * 16
+                nc.vector.tensor_copy(
+                    kw_got[j][:], kw_pool[:, :reach].bitcast(U32).indirect(offsets[:, first : first + 16])
+                )
+            for j in range(2):
+                nc.vector.tensor_copy(
+                    parted[:, :, j * 256 : (j + 1) * 256],
+                    kw_got[j][:].bitcast(U16).rearrange("x (n o) -> x o n", o=D_PASSES),
+                )
             kw_use.append(parted)
-        quantise_values(0, first_turned, slice(0, 2))
         second_got = sb.tile([P, N], BF16, name="second_got", align_bytes=64)
         nc.vector.tensor_copy(second_got[:], v_second[:].indirect(offsets[:]))
 
         gate = {}
+        flip_bank = {(0, 0): 4, (0, 1): 5, (1, 0): 7, (1, 1): 1}
         for g in range(SLOT_PASSES):
             inner, flip = [], []
-            for h in range(Q_BLOCKS):
+            banks = [bank_tile(2 * g + h, [P, K_PASS], f"score{g}{h}") for h in range(Q_BLOCKS)]
+            steps = [(h, o) for h in range(Q_BLOCKS) for o in range(D_PASSES)]
+            if g == 0:
+                steps = [(h, o) for o in range(D_PASSES) for h in range(Q_BLOCKS)]
+            for h, o in steps:
                 qs = slice(h * P, (h + 1) * P)
-                bank = bank_tile(2 * g + h, [P, K_PASS], f"score{g}{h}")
-                for o in range(D_PASSES):
-                    nc.tensor.matmul_mx(
-                        bank[:],
-                        lhsT=q_codes[:, o, qs].bitcast(FP8X4),
-                        lhsT_scale=q_scales[:, o, qs],
-                        rhs=kw_use[g][:, o, :].bitcast(FP4X4),
-                        rhs_scale=ks_bytes[:, o * N + g * K_PASS : o * N + (g + 1) * K_PASS],
-                        start=(o == 0),
-                        stop=(o == D_PASSES - 1),
-                    )
+                nc.tensor.matmul_mx(
+                    banks[h][:],
+                    lhsT=q_codes[:, o, qs].bitcast(FP8X4),
+                    lhsT_scale=q_scales[:, o, qs],
+                    rhs=kw_use[g][:, o, :].bitcast(FP4X4),
+                    rhs_scale=ks_bytes[:, o * N + g * K_PASS : o * N + (g + 1) * K_PASS],
+                    start=(o == 0),
+                    stop=(o == D_PASSES - 1),
+                )
+            for h in range(Q_BLOCKS):
+                bank = banks[h]
                 inner.append(shared.tile([P, PACK, P], F32, name=f"inner{g}{h}", offset=4096 + 2048 * h, align_bytes=64))
                 nc.scalar.activation(
                     inner[h][:].rearrange("q t (c i) -> q c t i", i=PACK),
@@ -180,15 +195,19 @@ def tile_attend_sigm_cap_srtq256n1024t2048_kernel(tc, qT, k_words, k_scales, vT,
                     bias=zero[:],
                     scale=half_scale[:],
                 )
-                flip.append(bank_tile(4 * (1 - g) + h, [P, PACK, P], f"flip{g}{h}"))
+                flip.append(bank_tile(flip_bank[g, h], [P, PACK, P], f"flip{g}{h}"))
             if g == 0:
                 for h in range(Q_BLOCKS):
-                    outer = sb.tile([P, PACK, P], F32, name=f"outer{h}", align_bytes=64)
+                    outer = shared.tile([P, PACK, P], F32, name=f"outer{h}", offset=8192 + 2048 * h, align_bytes=64)
                     nc.scalar.activation(outer[:], inner[h][:], ACT.Sigmoid, bias=zero[:], scale=2.0)
                     for t in range(PACK):
                         nc.tensor.transpose(flip[h][:, t, :], outer[:, t, :], ident[:])
                     gate[g, h] = flip[h][:].rearrange("p t q -> p q t")
+                late_bank = bank_tile(0, [P, 2, P], "late_bank")
+                turn_pass(late_bank, first_got[1][:])
             else:
+                late_words = shared.tile([P, 3, P, 2], F32, name="late_words", offset=10240, align_bytes=64)
+                nc.scalar.copy(late_words[:, 0], late_bank[:].rearrange("p u e -> p e u"))
                 for h in range(Q_BLOCKS):
                     for t in range(PACK):
                         nc.tensor.transpose(flip[h][:, t, :], inner[h][:, t, :], ident[:])
@@ -199,8 +218,10 @@ def tile_attend_sigm_cap_srtq256n1024t2048_kernel(tc, qT, k_words, k_scales, vT,
                     )
                     gate[g, h] = outer[:]
 
-        second_turned = shared.tile([P, SLOT_PASSES, P, 2], F32, name="second_turned", offset=6144, align_bytes=64)
-        turn_values(1, second_got, second_turned, 3)
+        second_bank = bank_tile(3, [P, SLOT_PASSES, 2, P], "second_bank")
+        for g in range(SLOT_PASSES):
+            turn_pass(second_bank[:, g], second_got[:, g * K_PASS : (g + 1) * K_PASS])
+        nc.scalar.copy(late_words[:, 1:3], second_bank[:].rearrange("p g u e -> p g e u"))
         w_bf = sb.tile([P, SLOT_PASSES, Q_BLOCKS, P, PACK], BF16, name="w_bf", align_bytes=64)
         w_codes = sb.tile([P, SLOT_PASSES, Q_BLOCKS, P], U32, name="w_codes", align_bytes=64)
         w_scales = sb.tile([P, SLOT_PASSES, Q_BLOCKS, P], U8, name="w_scales", align_bytes=64)
@@ -227,22 +248,24 @@ def tile_attend_sigm_cap_srtq256n1024t2048_kernel(tc, qT, k_words, k_scales, vT,
         quantise_weights(0, 1)
         weights(1, 1)
         quantise_weights(1, 0)
-        quantise_values(1, second_turned, slice(0, 2))
+        quantise_values(1, late_words[:, 0:2])
+        quantise_values(3, late_words[:, 2:3])
         quantise_weights(1, 1)
 
-        acc_bank = {(0, 0): 2, (0, 1): 6, (1, 0): 7, (1, 1): 4}
+        acc_bank = {(0, 0): 2, (0, 1): 6, (1, 0): 0, (1, 1): 4}
         for h in range(Q_BLOCKS):
             qs = slice(h * P, (h + 1) * P)
             result = sb.tile([P, V_BLOCKS, P], F32, name=f"result{h}")
             accs = [bank_tile(acc_bank[h, b], [P, P], f"acc{h}{b}") for b in range(V_BLOCKS)]
             for b in range(V_BLOCKS):
                 for g in range(SLOT_PASSES):
+                    cols = slice((SLOT_PASSES * b + g) * P, (SLOT_PASSES * b + g + 1) * P)
                     nc.tensor.matmul_mx(
                         accs[b][:],
                         lhsT=w_codes[:, g, h].bitcast(FP8X4),
                         lhsT_scale=w_scales[:, g, h],
-                        rhs=v_codes[:, b, g].bitcast(FP8X4),
-                        rhs_scale=v_scales[:, b, g],
+                        rhs=v_codes[:, cols].bitcast(FP8X4),
+                        rhs_scale=v_scales[:, cols],
                         start=(g == 0),
                         stop=(g == SLOT_PASSES - 1),
                     )

@@ -90,7 +90,7 @@ def tile_attend_sigm_cap_srtq256n1024t2048_kernel(tc, qT, k_words, k_scales, vT,
         v_second = sb.tile([P, T], F32, name="v_second", align_bytes=64)
         nc.sync.dma_start(v_second[:], vT[P : 2 * P, :])
 
-        vs_got = sb.tile([P, N], F32, name="vs_got")
+        vs_got = shared.tile([P, N], F32, name="vs_got", offset=16384, align_bytes=64)
         nc.vector.tensor_copy(vs_got[:], vs_pool[:].indirect(offsets[:]))
         vs_col = [sb.tile([P, PACK], F32, name=f"vs_col{g}") for g in range(SLOT_PASSES)]
         for g in range(SLOT_PASSES):
@@ -187,7 +187,7 @@ def tile_attend_sigm_cap_srtq256n1024t2048_kernel(tc, qT, k_words, k_scales, vT,
                 )
             for h in range(Q_BLOCKS):
                 bank = banks[h]
-                inner.append(shared.tile([P, PACK, P], F32, name=f"inner{g}{h}", offset=4096 + 2048 * h, align_bytes=64))
+                inner.append(shared.tile([P, PACK, P], F32, name=f"inner{g}{h}", offset=4096 + 12288 * g + 2048 * h, align_bytes=64))
                 nc.scalar.activation(
                     inner[h][:].rearrange("q t (c i) -> q c t i", i=PACK),
                     bank[:].rearrange("q (c i t) -> q c t i", i=PACK, t=PACK),
@@ -203,11 +203,12 @@ def tile_attend_sigm_cap_srtq256n1024t2048_kernel(tc, qT, k_words, k_scales, vT,
                     for t in range(PACK):
                         nc.tensor.transpose(flip[h][:, t, :], outer[:, t, :], ident[:])
                     gate[g, h] = flip[h][:].rearrange("p t q -> p q t")
-                late_bank = bank_tile(0, [P, 2, P], "late_bank")
-                turn_pass(late_bank, first_got[1][:])
+                late_bank = bank_tile(0, [P, 2, 2, P], "late_bank")
+                turn_pass(late_bank[:, 0], first_got[1][:])
+                turn_pass(late_bank[:, 1], second_got[:, :K_PASS])
             else:
-                late_words = shared.tile([P, 3, P, 2], F32, name="late_words", offset=10240, align_bytes=64)
-                nc.scalar.copy(late_words[:, 0], late_bank[:].rearrange("p u e -> p e u"))
+                late_words = sb.tile([P, 2, P, 2], F32, name="late_words", align_bytes=64)
+                nc.scalar.copy(late_words[:], late_bank[:].rearrange("p g u e -> p g e u"))
                 for h in range(Q_BLOCKS):
                     for t in range(PACK):
                         nc.tensor.transpose(flip[h][:, t, :], inner[h][:, t, :], ident[:])
@@ -218,10 +219,10 @@ def tile_attend_sigm_cap_srtq256n1024t2048_kernel(tc, qT, k_words, k_scales, vT,
                     )
                     gate[g, h] = outer[:]
 
-        second_bank = bank_tile(3, [P, SLOT_PASSES, 2, P], "second_bank")
-        for g in range(SLOT_PASSES):
-            turn_pass(second_bank[:, g], second_got[:, g * K_PASS : (g + 1) * K_PASS])
-        nc.scalar.copy(late_words[:, 1:3], second_bank[:].rearrange("p g u e -> p g e u"))
+        last_bank = bank_tile(3, [P, 2, P], "last_bank")
+        turn_pass(last_bank, second_got[:, K_PASS:])
+        last_words = sb.tile([P, 1, P, 2], F32, name="last_words", align_bytes=64)
+        nc.scalar.copy(last_words[:, 0], last_bank[:].rearrange("p u e -> p e u"))
         w_bf = sb.tile([P, SLOT_PASSES, Q_BLOCKS, P, PACK], BF16, name="w_bf", align_bytes=64)
         w_codes = sb.tile([P, SLOT_PASSES, Q_BLOCKS, P], U32, name="w_codes", align_bytes=64)
         w_scales = sb.tile([P, SLOT_PASSES, Q_BLOCKS, P], U8, name="w_scales", align_bytes=64)
@@ -244,12 +245,12 @@ def tile_attend_sigm_cap_srtq256n1024t2048_kernel(tc, qT, k_words, k_scales, vT,
         weights(0, 0)
         weights(0, 1)
         quantise_weights(0, 0)
-        weights(1, 0)
         quantise_weights(0, 1)
+        quantise_values(1, late_words[:])
+        weights(1, 0)
         weights(1, 1)
         quantise_weights(1, 0)
-        quantise_values(1, late_words[:, 0:2])
-        quantise_values(3, late_words[:, 2:3])
+        quantise_values(3, last_words[:])
         quantise_weights(1, 1)
 
         acc_bank = {(0, 0): 2, (0, 1): 6, (1, 0): 0, (1, 1): 4}

@@ -42,7 +42,7 @@ def tile_attend_sigm_cap_srtq256n1024t2048_kernel(tc, qT, k_words, k_scales, vT,
         q_dram = qT[0].rearrange("(o p j) q -> o p j q", o=D_PASSES, j=PACK)
         q_raw = [sb.tile([P, PACK, NQ], F32, name=f"q_raw{o}", tag=f"queries{o}", align_bytes=64) for o in range(D_PASSES)]
         v_first = sb.tile([P, T], F32, name="v_first", align_bytes=64)
-        pieces = [slice(0, 1024), slice(1024, 1536), slice(1536, T)]
+        pieces = [slice(0, 768), slice(768, 1536), slice(1536, T)]
         for cols in pieces[:2]:
             nc.sync.dma_start(v_first[:, cols], vT[0:P, cols])
         nc.gpsimd.memset(ks_pool[0:96, :], 0)
@@ -88,9 +88,10 @@ def tile_attend_sigm_cap_srtq256n1024t2048_kernel(tc, qT, k_words, k_scales, vT,
 
         nc.sync.dma_start(kw_pool[:, 1536:], kw_dram[:, 1536:])
         v_second = sb.tile([P, T], F32, name="v_second", align_bytes=64)
-        nc.sync.dma_start(v_second[:], vT[P : 2 * P, :])
+        nc.sync.dma_start(v_second[:, :1536], vT[P : 2 * P, :1536])
+        nc.sync.dma_start(v_second[:, 1536:], vT[P : 2 * P, 1536:])
 
-        vs_got = shared.tile([P, N], F32, name="vs_got", offset=16384, align_bytes=64)
+        vs_got = sb.tile([P, N], F32, name="vs_got", align_bytes=64)
         nc.vector.tensor_copy(vs_got[:], vs_pool[:].indirect(offsets[:]))
         vs_col = [sb.tile([P, PACK], F32, name=f"vs_col{g}") for g in range(SLOT_PASSES)]
         for g in range(SLOT_PASSES):
@@ -101,7 +102,7 @@ def tile_attend_sigm_cap_srtq256n1024t2048_kernel(tc, qT, k_words, k_scales, vT,
         q_bf = sb.tile([P, D_PASSES, NQ, PACK], BF16, name="q_bf", align_bytes=64)
         woven = [q_bf[:, o].rearrange("p (c i) j -> p c j i", i=PACK) for o in range(D_PASSES)]
         rows = [q_raw[o][:].rearrange("p j (c i) -> p c j i", i=PACK) for o in range(D_PASSES)]
-        half = NQ // PACK // 2
+        half = NQ // PACK // 4
 
         v_bf = sb.tile([P, T], BF16, name="v_bf", align_bytes=64)
         for cols in pieces[:2]:
@@ -130,11 +131,10 @@ def tile_attend_sigm_cap_srtq256n1024t2048_kernel(tc, qT, k_words, k_scales, vT,
         early_bank = bank_tile(6, [P, 2, P], "early_bank")
         for u in range(2):
             nc.tensor.transpose(early_bank[:, u, :], first_got[0][:].bitcast(F32)[:, u * P : (u + 1) * P], ident[:])
-        early_words = sb.tile([P, 1, P, 2], F32, name="early_words", tag="queries0", align_bytes=64)
-        nc.scalar.copy(early_words[:, 0], early_bank[:].rearrange("p u e -> p e u"))
+        early_words = sb.tile([P, 1, P, 2], F32, name="early_words", tag="queries1", align_bytes=64)
         nc.scalar.activation(v_bf[:, pieces[2]], v_first[:, pieces[2]], ACT.Copy)
+        nc.scalar.copy(early_words[:, 0], early_bank[:].rearrange("p u e -> p e u"))
         nc.scalar.activation(first_got[1][:], v_bf[:].indirect(offsets[:, 32:64]), ACT.Copy)
-        v_codes = sb.tile([P, V_BLOCKS * SLOT_PASSES * P], U32, name="v_codes", align_bytes=64)
         v_scales = sb.tile([P, V_BLOCKS * SLOT_PASSES * P], U8, name="v_scales", align_bytes=64)
 
         def quantise_values(first, v_words):
@@ -145,13 +145,14 @@ def tile_attend_sigm_cap_srtq256n1024t2048_kernel(tc, qT, k_words, k_scales, vT,
                 in_=v_words.rearrange("p g e u -> p (g e u)").bitcast(BF16),
             )
 
-        quantise_values(0, early_words[:])
-
         kw_use = []
         for g in range(SLOT_PASSES):
             reach = T - N + (g + 1) * K_PASS
             parted = sb.tile([P, D_PASSES, K_PASS], U16, name=f"kw_use{g}", align_bytes=64)
-            kw_got = [sb.tile([P, 256], U32, name=f"kw_got{g}{j}", align_bytes=64) for j in range(2)]
+            kw_got = [
+                shared.tile([P, 256], U32, name=f"kw_got{g}{j}", offset=24576 + 2048 * (2 * g + j), align_bytes=64)
+                for j in range(2)
+            ]
             for j in range(2):
                 first = g * 32 + j * 16
                 nc.vector.tensor_copy(
@@ -163,8 +164,14 @@ def tile_attend_sigm_cap_srtq256n1024t2048_kernel(tc, qT, k_words, k_scales, vT,
                     kw_got[j][:].bitcast(U16).rearrange("x (n o) -> x o n", o=D_PASSES),
                 )
             kw_use.append(parted)
-        second_got = sb.tile([P, N], BF16, name="second_got", align_bytes=64)
-        nc.vector.tensor_copy(second_got[:], v_second[:].indirect(offsets[:]))
+        v_codes = shared.tile([P, V_BLOCKS * SLOT_PASSES * P], U32, name="v_codes", offset=28672, align_bytes=64)
+        quantise_values(0, early_words[:])
+        second_got = [sb.tile([P, K_PASS], BF16, name=f"second_got{g}", align_bytes=64) for g in range(SLOT_PASSES)]
+        nc.vector.tensor_copy(
+            second_got[0][:].rearrange("p (u s e) -> p s u e", u=2, e=2),
+            v_second[:, :1536].indirect(offsets[:, 0:32]),
+        )
+        nc.vector.tensor_copy(second_got[1][:], v_second[:].indirect(offsets[:, 32:64]))
 
         gate = {}
         flip_bank = {(0, 0): 4, (0, 1): 5, (1, 0): 7, (1, 1): 1}
@@ -187,7 +194,7 @@ def tile_attend_sigm_cap_srtq256n1024t2048_kernel(tc, qT, k_words, k_scales, vT,
                 )
             for h in range(Q_BLOCKS):
                 bank = banks[h]
-                inner.append(shared.tile([P, PACK, P], F32, name=f"inner{g}{h}", offset=4096 + 12288 * g + 2048 * h, align_bytes=64))
+                inner.append(shared.tile([P, PACK, P], F32, name=f"inner{g}{h}", offset=4096 + 2048 * h, align_bytes=64))
                 nc.scalar.activation(
                     inner[h][:].rearrange("q t (c i) -> q c t i", i=PACK),
                     bank[:].rearrange("q (c i t) -> q c t i", i=PACK, t=PACK),
@@ -205,7 +212,10 @@ def tile_attend_sigm_cap_srtq256n1024t2048_kernel(tc, qT, k_words, k_scales, vT,
                     gate[g, h] = flip[h][:].rearrange("p t q -> p q t")
                 late_bank = bank_tile(0, [P, 2, 2, P], "late_bank")
                 turn_pass(late_bank[:, 0], first_got[1][:])
-                turn_pass(late_bank[:, 1], second_got[:, :K_PASS])
+                for u in range(2):
+                    nc.tensor.transpose(
+                        late_bank[:, 1, u, :], second_got[0][:].bitcast(F32)[:, u * P : (u + 1) * P], ident[:]
+                    )
             else:
                 late_words = sb.tile([P, 2, P, 2], F32, name="late_words", align_bytes=64)
                 nc.scalar.copy(late_words[:], late_bank[:].rearrange("p g u e -> p g e u"))
@@ -220,7 +230,7 @@ def tile_attend_sigm_cap_srtq256n1024t2048_kernel(tc, qT, k_words, k_scales, vT,
                     gate[g, h] = outer[:]
 
         last_bank = bank_tile(3, [P, 2, P], "last_bank")
-        turn_pass(last_bank, second_got[:, K_PASS:])
+        turn_pass(last_bank, second_got[1][:])
         last_words = sb.tile([P, 1, P, 2], F32, name="last_words", align_bytes=64)
         nc.scalar.copy(last_words[:, 0], last_bank[:].rearrange("p u e -> p e u"))
         w_bf = sb.tile([P, SLOT_PASSES, Q_BLOCKS, P, PACK], BF16, name="w_bf", align_bytes=64)
@@ -246,10 +256,10 @@ def tile_attend_sigm_cap_srtq256n1024t2048_kernel(tc, qT, k_words, k_scales, vT,
         weights(0, 1)
         quantise_weights(0, 0)
         quantise_weights(0, 1)
-        quantise_values(1, late_words[:])
         weights(1, 0)
-        weights(1, 1)
+        quantise_values(1, late_words[:])
         quantise_weights(1, 0)
+        weights(1, 1)
         quantise_values(3, last_words[:])
         quantise_weights(1, 1)
 

@@ -41,7 +41,7 @@ def tile_attend_sigm_cap_srtq256n1024t2048_kernel(tc, qT, k_words, k_scales, vT,
         nc.sync.dma_start(offsets[:], offs)
         q_dram = qT[0].rearrange("(o p j) q -> o p j q", o=D_PASSES, j=PACK)
         q_raw = [sb.tile([P, PACK, NQ], F32, name=f"q_raw{o}", tag=f"queries{o}", align_bytes=64) for o in range(D_PASSES)]
-        v_first = sb.tile([P, T], F32, name="v_first", align_bytes=64)
+        v_first = shared.tile([P, T], F32, name="v_first", offset=0, align_bytes=64)
         pieces = [slice(0, 768), slice(768, 1536), slice(1536, T)]
         for cols in pieces[:2]:
             nc.sync.dma_start(v_first[:, cols], vT[0:P, cols])
@@ -75,7 +75,6 @@ def tile_attend_sigm_cap_srtq256n1024t2048_kernel(tc, qT, k_words, k_scales, vT,
         nc.sync.dma_start(kw_pool[:, :1536], kw_dram[:, :1536])
         nc.sync.dma_start(q_raw[0][:], q_dram[0])
         nc.sync.dma_start(q_raw[1][:], q_dram[1])
-        nc.sync.dma_start(v_first[:, pieces[2]], vT[0:P, pieces[2]])
 
         ks_got = sb.tile([P, N], U8, name="ks_got", align_bytes=64)
         nc.vector.tensor_copy(ks_got[:], ks_pool[:].bitcast(U8).indirect(offsets[:]))
@@ -86,6 +85,7 @@ def tile_attend_sigm_cap_srtq256n1024t2048_kernel(tc, qT, k_words, k_scales, vT,
             )
         ks_bytes = ks_use[:].rearrange("x o n -> x (o n)").bitcast(U8)
 
+        nc.sync.dma_start(v_first[:, pieces[2]], vT[0:P, pieces[2]])
         nc.sync.dma_start(kw_pool[:, 1536:], kw_dram[:, 1536:])
         v_second = sb.tile([P, T], F32, name="v_second", align_bytes=64)
         nc.sync.dma_start(v_second[:, :1536], vT[P : 2 * P, :1536])

@@ -32,6 +32,9 @@ def tile_attend_sigm_cap_srtq256n1024t2048_kernel(tc, qT, k_words, k_scales, vT,
         shared = ctx.enter_context(tc.tile_pool(name="shared", bufs=1))
         ps = ctx.enter_context(tc.psum_pool(name="ps", bufs=1))
 
+        def dealt(tile):
+            return tile[:].rearrange("p (u s e) -> p s u e", u=2, e=2)
+
         def bank_tile(number, shape, name):
             return ps.tile(shape, F32, name=name, offset=2048 * number)
 
@@ -126,7 +129,7 @@ def tile_attend_sigm_cap_srtq256n1024t2048_kernel(tc, qT, k_words, k_scales, vT,
         def turn_pass(bank, got):
             words = got.bitcast(F32)
             for u in range(2):
-                nc.tensor.transpose(bank[:, u, :], words[:, u::2], ident[:])
+                nc.tensor.transpose(bank[:, u, :], words[:, u * P : (u + 1) * P], ident[:])
 
         early_bank = bank_tile(6, [P, 2, P], "early_bank")
         for u in range(2):
@@ -134,7 +137,7 @@ def tile_attend_sigm_cap_srtq256n1024t2048_kernel(tc, qT, k_words, k_scales, vT,
         early_words = sb.tile([P, 1, P, 2], F32, name="early_words", tag="queries1", align_bytes=64)
         nc.scalar.activation(v_bf[:, pieces[2]], v_first[:, pieces[2]], ACT.Copy)
         nc.scalar.copy(early_words[:, 0], early_bank[:].rearrange("p u e -> p e u"))
-        nc.scalar.activation(first_got[1][:], v_bf[:].indirect(offsets[:, 32:64]), ACT.Copy)
+        nc.scalar.activation(dealt(first_got[1]), v_bf[:].indirect(offsets[:, 32:64]), ACT.Copy)
         v_scales = sb.tile([P, V_BLOCKS * SLOT_PASSES * P], U8, name="v_scales", align_bytes=64)
 
         def quantise_values(first, v_words):
@@ -171,7 +174,7 @@ def tile_attend_sigm_cap_srtq256n1024t2048_kernel(tc, qT, k_words, k_scales, vT,
             second_got[0][:].rearrange("p (u s e) -> p s u e", u=2, e=2),
             v_second[:, :1536].indirect(offsets[:, 0:32]),
         )
-        nc.vector.tensor_copy(second_got[1][:], v_second[:].indirect(offsets[:, 32:64]))
+        nc.vector.tensor_copy(dealt(second_got[1]), v_second[:].indirect(offsets[:, 32:64]))
 
         gate = {}
         flip_bank = {(0, 0): 4, (0, 1): 5, (1, 0): 7, (1, 1): 1}

@@ -77,19 +77,28 @@ def tile_attend_sigm_cap_srtq256n1024t2048_kernel(tc, qT, k_words, k_scales, vT,
         kw_dram = k_words[0].rearrange("p t b -> p (t b)").bitcast(I32)
         nc.sync.dma_start(kw_pool[:, :1536], kw_dram[:, :1536])
         nc.sync.dma_start(q_raw[0][:], q_dram[0])
-        nc.sync.dma_start(q_raw[1][:], q_dram[1])
 
-        ks_got = sb.tile([P, N], U8, name="ks_got", align_bytes=64)
-        nc.vector.tensor_copy(ks_got[:], ks_pool[:].bitcast(U8).indirect(offsets[:]))
-        for quad in range(4):
-            nc.sync.dma_start(
-                ks_use[32 * quad : 32 * quad + 4, :, :],
-                ks_got[96 + 8 * quad : 104 + 8 * quad, :].bitcast(I32),
+        ks_got = shared.tile([P, N], U8, name="ks_got", offset=16384, align_bytes=64)
+        for g in range(SLOT_PASSES):
+            nc.vector.tensor_copy(
+                ks_got[:, g * K_PASS : (g + 1) * K_PASS],
+                ks_pool[:].bitcast(U8).indirect(offsets[:, 32 * g : 32 * g + 32]),
             )
+
+        def move_scale_rows(g):
+            for quad in range(4):
+                nc.sync.dma_start(
+                    ks_use[32 * quad : 32 * quad + 4, :, g * P : (g + 1) * P],
+                    ks_got[96 + 8 * quad : 104 + 8 * quad, g * K_PASS : (g + 1) * K_PASS].bitcast(I32),
+                )
+
+        move_scale_rows(0)
+        nc.sync.dma_start(q_raw[1][:], q_dram[1])
         ks_bytes = ks_use[:].rearrange("x o n -> x (o n)").bitcast(U8)
 
         nc.sync.dma_start(v_first[:, pieces[2]], vT[0:P, pieces[2]])
         nc.sync.dma_start(kw_pool[:, 1536:], kw_dram[:, 1536:])
+        move_scale_rows(1)
         v_second = sb.tile([P, T], F32, name="v_second", align_bytes=64)
         nc.sync.dma_start(v_second[:, :1536], vT[P : 2 * P, :1536])
         nc.sync.dma_start(v_second[:, 1536:], vT[P : 2 * P, 1536:])
@@ -197,7 +206,7 @@ def tile_attend_sigm_cap_srtq256n1024t2048_kernel(tc, qT, k_words, k_scales, vT,
                 )
             for h in range(Q_BLOCKS):
                 bank = banks[h]
-                inner.append(shared.tile([P, PACK, P], F32, name=f"inner{g}{h}", offset=4096 + 2048 * h, align_bytes=64))
+                inner.append(shared.tile([P, PACK, P], F32, name=f"inner{g}{h}", offset=(16384, 6144)[h], align_bytes=64))
                 nc.scalar.activation(
                     inner[h][:].rearrange("q t (c i) -> q c t i", i=PACK),
                     bank[:].rearrange("q (c i t) -> q c t i", i=PACK, t=PACK),

from contextlib import ExitStack

import concourse.mybir as mybir

N, T, D, DV, NQ = 1024, 2048, 1024, 256, 256
FLOPS = 2 * NQ * N * D + 2 * NQ * N * DV

F32 = mybir.dt.float32
BF16 = mybir.dt.bfloat16
I32 = mybir.dt.int32
U32 = mybir.dt.uint32
U16 = mybir.dt.uint16
U8 = mybir.dt.uint8
FP8X4 = mybir.dt.float8_e4m3fn_x4
FP4X4 = mybir.dt.float4_e2m1fn_x4
ACT = mybir.ActivationFunctionType
ALU = mybir.AluOpType

P = 128
PACK = 4
K_PASS = P * PACK
D_PASSES = D // K_PASS
SLOT_PASSES = N // K_PASS
Q_BLOCKS = NQ // P
V_BLOCKS = DV // P


def tile_attend_sigm_cap_srtq256n1024t2048_kernel(tc, qT, k_words, k_scales, vT, vs, offs, out):
    nc = tc.nc
    with ExitStack() as ctx:
        sb = ctx.enter_context(tc.tile_pool(name="sb", bufs=1))
        shared = ctx.enter_context(tc.tile_pool(name="shared", bufs=1))
        ps = ctx.enter_context(tc.psum_pool(name="ps", bufs=1))

        def dealt(tile):
            return tile[:].rearrange("p (u s e) -> p s u e", u=2, e=2)

        def bank_tile(number, shape, name):
            return ps.tile(shape, F32, name=name, offset=2048 * number)

        offsets = sb.tile([P, N // 16], U16, name="offsets")
        ks_pool = sb.tile([P, T // 4], I32, name="ks_pool", align_bytes=64)
        nc.sync.dma_start(ks_pool[96:128, :], k_scales.rearrange("o f t -> f o t").bitcast(I32))
        nc.sync.dma_start(offsets[:], offs)
        q_dram = qT[0].rearrange("(o p j) q -> o p j q", o=D_PASSES, j=PACK)
        q_raw = [sb.tile([P, PACK, NQ], F32, name=f"q_raw{o}", tag=f"queries{o}", align_bytes=64) for o in range(D_PASSES)]
        v_first = shared.tile([P, T], F32, name="v_first", offset=0, align_bytes=64)
        pieces = [slice(0, 768), slice(768, 1536), slice(1536, T)]
        for cols in pieces[:2]:
            nc.sync.dma_start(v_first[:, cols], vT[0:P, cols])
        nc.gpsimd.memset(ks_pool[0:96, :], 0)
        vs_pool = sb.tile([P, T], F32, name="vs_pool", align_bytes=64)
        nc.gpsimd.memset(vs_pool[:, :1024], 0.0)
        nc.vector.memset(vs_pool[:, 1024:1535], 0.0)
        nc.vector.memset(vs_pool[:, 1535:], 0.0)
        nc.sync.dma_start(vs_pool[0:1, :], vs[0:1, :])
        zero = sb.tile([P, 1], F32, name="zero")
        nc.vector.memset(zero[:], 0.0)
        half_scale = sb.tile([P, 1], F32, name="half_scale")
        nc.scalar.activation(half_scale[:], zero[:], ACT.Sigmoid, bias=zero[:])
        ks_use = sb.tile([P, D_PASSES, N // 4], I32, name="ks_use", align_bytes=64)
        nc.gpsimd.memset(ks_use[:], 0)
        blank = sb.tile([P, P], F32, name="blank", align_bytes=64)
        nc.gpsimd.memset(blank[:], 0.0)
        ident = sb.tile([P, P], F32, name="ident")
        nc.gpsimd.affine_select(
            out=ident[:],
            in_=blank[:],
            compare_op=ALU.not_equal,
            fill=1.0,
            base=0,
            pattern=[[-1, P]],
            channel_multiplier=1,
        )

        kw_pool = sb.tile([P, T], I32, name="kw_pool", align_bytes=64)
        kw_dram = k_words[0].rearrange("p t b -> p (t b)").bitcast(I32)
        nc.sync.dma_start(kw_pool[:, :1536], kw_dram[:, :1536])
        nc.sync.dma_start(q_raw[0][:], q_dram[0])

        ks_got = shared.tile([P, N], U8, name="ks_got", offset=16384, align_bytes=64)
        for g in range(SLOT_PASSES):
            nc.vector.tensor_copy(
                ks_got[:, g * K_PASS : (g + 1) * K_PASS],
                ks_pool[:].bitcast(U8).indirect(offsets[:, 32 * g : 32 * g + 32]),
            )

        def move_scale_rows(g):
            for quad in range(4):
                nc.sync.dma_start(
                    ks_use[32 * quad : 32 * quad + 4, :, g * P : (g + 1) * P],
                    ks_got[96 + 8 * quad : 104 + 8 * quad, g * K_PASS : (g + 1) * K_PASS].bitcast(I32),
                )

        move_scale_rows(0)
        nc.sync.dma_start(q_raw[1][:], q_dram[1])
        ks_bytes = ks_use[:].rearrange("x o n -> x (o n)").bitcast(U8)

        nc.sync.dma_start(v_first[:, pieces[2]], vT[0:P, pieces[2]])
        nc.sync.dma_start(kw_pool[:, 1536:], kw_dram[:, 1536:])
        move_scale_rows(1)
        v_second = sb.tile([P, T], F32, name="v_second", align_bytes=64)
        nc.sync.dma_start(v_second[:, :1536], vT[P : 2 * P, :1536])
        nc.sync.dma_start(v_second[:, 1536:], vT[P : 2 * P, 1536:])

        vs_got = sb.tile([P, N], F32, name="vs_got", align_bytes=64)
        nc.vector.tensor_copy(vs_got[:], vs_pool[:].indirect(offsets[:]))
        vs_col = [sb.tile([P, PACK], F32, name=f"vs_col{g}") for g in range(SLOT_PASSES)]
        for g in range(SLOT_PASSES):
            nc.sync.dma_start(vs_col[g][:], vs_got[0:1, g * K_PASS : (g + 1) * K_PASS])

        q_codes = sb.tile([P, D_PASSES, NQ], U32, name="q_codes", align_bytes=64)
        q_scales = sb.tile([P, D_PASSES, NQ], U8, name="q_scales", align_bytes=64)
        q_bf = sb.tile([P, D_PASSES, NQ, PACK], BF16, name="q_bf", align_bytes=64)
        woven = [q_bf[:, o].rearrange("p (c i) j -> p c j i", i=PACK) for o in range(D_PASSES)]
        rows = [q_raw[o][:].rearrange("p j (c i) -> p c j i", i=PACK) for o in range(D_PASSES)]
        half = NQ // PACK // 4

        v_bf = sb.tile([P, T], BF16, name="v_bf", align_bytes=64)
        for cols in pieces[:2]:
            nc.scalar.activation(v_bf[:, cols], v_first[:, cols], ACT.Copy)
        first_got = [sb.tile([P, K_PASS], BF16, name=f"first_got{g}", align_bytes=64) for g in range(SLOT_PASSES)]
        nc.scalar.activation(
            first_got[0][:].rearrange("p (u s e) -> p s u e", u=2, e=2),
            v_bf[:, :1536].indirect(offsets[:, 0:32]),
            ACT.Copy,
        )
        nc.scalar.copy(woven[0], rows[0])
        nc.vector.tensor_copy(woven[1][:, :half], rows[1][:, :half])
        nc.scalar.copy(woven[1][:, half:], rows[1][:, half:])
        for o in range(D_PASSES):
            nc.vector.quantize_mx(
                out=q_codes[:, o].bitcast(FP8X4),
                scales=q_scales[:, o],
                in_=q_bf[:, o].rearrange("p q j -> p (q j)"),
            )

        def turn_pass(bank, got):
            words = got.bitcast(F32)
            for u in range(2):
                nc.tensor.transpose(bank[:, u, :], words[:, u * P : (u + 1) * P], ident[:])

        early_bank = bank_tile(6, [P, 2, P], "early_bank")
        for u in range(2):
            nc.tensor.transpose(early_bank[:, u, :], first_got[0][:].bitcast(F32)[:, u * P : (u + 1) * P], ident[:])
        early_words = sb.tile([P, 1, P, 2], F32, name="early_words", tag="queries1", align_bytes=64)
        nc.scalar.activation(v_bf[:, pieces[2]], v_first[:, pieces[2]], ACT.Copy)
        nc.scalar.copy(early_words[:, 0], early_bank[:].rearrange("p u e -> p e u"))
        nc.scalar.activation(dealt(first_got[1]), v_bf[:].indirect(offsets[:, 32:64]), ACT.Copy)
        v_scales = sb.tile([P, V_BLOCKS * SLOT_PASSES * P], U8, name="v_scales", align_bytes=64)

        def quantise_values(first, v_words):
            cols = slice(first * P, (first + v_words.shape[1]) * P)
            nc.vector.quantize_mx(
                out=v_codes[:, cols].bitcast(FP8X4),
                scales=v_scales[:, cols],
                in_=v_words.rearrange("p g e u -> p (g e u)").bitcast(BF16),
            )

        kw_use = []
        for g in range(SLOT_PASSES):
            reach = T - N + (g + 1) * K_PASS
            parted = sb.tile([P, D_PASSES, K_PASS], U16, name=f"kw_use{g}", align_bytes=64)
            kw_got = [
                shared.tile([P, 256], U32, name=f"kw_got{g}{j}", offset=24576 + 2048 * (2 * g + j), align_bytes=64)
                for j in range(2)
            ]
            for j in range(2):
                first = g * 32 + j * 16
                nc.vector.tensor_copy(
                    kw_got[j][:], kw_pool[:, :reach].bitcast(U32).indirect(offsets[:, first : first + 16])
                )
            for j in range(2):
                nc.vector.tensor_copy(
                    parted[:, :, j * 256 : (j + 1) * 256],
                    kw_got[j][:].bitcast(U16).rearrange("x (n o) -> x o n", o=D_PASSES),
                )
            kw_use.append(parted)
        v_codes = shared.tile([P, V_BLOCKS * SLOT_PASSES * P], U32, name="v_codes", offset=28672, align_bytes=64)
        quantise_values(0, early_words[:])
        second_got = [sb.tile([P, K_PASS], BF16, name=f"second_got{g}", align_bytes=64) for g in range(SLOT_PASSES)]
        nc.vector.tensor_copy(
            second_got[0][:].rearrange("p (u s e) -> p s u e", u=2, e=2),
            v_second[:, :1536].indirect(offsets[:, 0:32]),
        )
        nc.vector.tensor_copy(dealt(second_got[1]), v_second[:].indirect(offsets[:, 32:64]))

        gate = {}
        flip_bank = {(0, 0): 4, (0, 1): 5, (1, 0): 7, (1, 1): 1}
        for g in range(SLOT_PASSES):
            inner, flip = [], []
            banks = [bank_tile(2 * g + h, [P, K_PASS], f"score{g}{h}") for h in range(Q_BLOCKS)]
            steps = [(h, o) for h in range(Q_BLOCKS) for o in range(D_PASSES)]
            if g == 0:
                steps = [(h, o) for o in range(D_PASSES) for h in range(Q_BLOCKS)]
            for h, o in steps:
                qs = slice(h * P, (h + 1) * P)
                nc.tensor.matmul_mx(
                    banks[h][:],
                    lhsT=q_codes[:, o, qs].bitcast(FP8X4),
                    lhsT_scale=q_scales[:, o, qs],
                    rhs=kw_use[g][:, o, :].bitcast(FP4X4),
                    rhs_scale=ks_bytes[:, o * N + g * K_PASS : o * N + (g + 1) * K_PASS],
                    start=(o == 0),
                    stop=(o == D_PASSES - 1),
                )
            for h in range(Q_BLOCKS):
                bank = banks[h]
                inner.append(shared.tile([P, PACK, P], F32, name=f"inner{g}{h}", offset=(16384, 6144)[h], align_bytes=64))
                nc.scalar.activation(
                    inner[h][:].rearrange("q t (c i) -> q c t i", i=PACK),
                    bank[:].rearrange("q (c i t) -> q c t i", i=PACK, t=PACK),
                    ACT.Tanh,
                    bias=zero[:],
                    scale=half_scale[:],
                )
                flip.append(bank_tile(flip_bank[g, h], [P, PACK, P], f"flip{g}{h}"))
            if g == 0:
                for h in range(Q_BLOCKS):
                    outer = shared.tile([P, PACK, P], F32, name=f"outer{h}", offset=8192 + 2048 * h, align_bytes=64)
                    nc.scalar.activation(outer[:], inner[h][:], ACT.Sigmoid, bias=zero[:], scale=2.0)
                    for t in range(PACK):
                        nc.tensor.transpose(flip[h][:, t, :], outer[:, t, :], ident[:])
                    gate[g, h] = flip[h][:].rearrange("p t q -> p q t")
                late_bank = bank_tile(0, [P, 2, 2, P], "late_bank")
                turn_pass(late_bank[:, 0], first_got[1][:])
                for u in range(2):
                    nc.tensor.transpose(
                        late_bank[:, 1, u, :], second_got[0][:].bitcast(F32)[:, u * P : (u + 1) * P], ident[:]
                    )
            else:
                late_words = sb.tile([P, 2, P, 2], F32, name="late_words", align_bytes=64)
                nc.scalar.copy(late_words[:], late_bank[:].rearrange("p g u e -> p g e u"))
                for h in range(Q_BLOCKS):
                    for t in range(PACK):
                        nc.tensor.transpose(flip[h][:, t, :], inner[h][:, t, :], ident[:])
                for h in range(Q_BLOCKS):
                    outer = sb.tile([P, P, PACK], F32, name=f"gate{h}", align_bytes=64)
                    nc.scalar.activation(
                        outer[:], flip[h][:].rearrange("p t q -> p q t"), ACT.Sigmoid, bias=zero[:], scale=2.0
                    )
                    gate[g, h] = outer[:]

        last_bank = bank_tile(3, [P, 2, P], "last_bank")
        turn_pass(last_bank, second_got[1][:])
        last_words = sb.tile([P, 1, P, 2], F32, name="last_words", align_bytes=64)
        nc.scalar.copy(last_words[:, 0], last_bank[:].rearrange("p u e -> p e u"))
        w_bf = sb.tile([P, SLOT_PASSES, Q_BLOCKS, P, PACK], BF16, name="w_bf", align_bytes=64)
        w_codes = sb.tile([P, SLOT_PASSES, Q_BLOCKS, P], U32, name="w_codes", align_bytes=64)
        w_scales = sb.tile([P, SLOT_PASSES, Q_BLOCKS, P], U8, name="w_scales", align_bytes=64)

        def weights(g, h):
            nc.vector.tensor_tensor(
                w_bf[:, g, h],
                gate[g, h],
                vs_col[g][:].unsqueeze(1).to_broadcast([P, P, PACK]),
                ALU.mult,
            )

        def quantise_weights(g, h):
            nc.vector.quantize_mx(
                out=w_codes[:, g, h].bitcast(FP8X4),
                scales=w_scales[:, g, h],
                in_=w_bf[:, g, h].rearrange("p q t -> p (q t)"),
            )

        weights(0, 0)
        weights(0, 1)
        quantise_weights(0, 0)
        quantise_weights(0, 1)
        weights(1, 0)
        quantise_values(1, late_words[:])
        quantise_weights(1, 0)
        weights(1, 1)
        quantise_values(3, last_words[:])
        quantise_weights(1, 1)

        acc_bank = {(0, 0): 2, (0, 1): 6, (1, 0): 0, (1, 1): 4}
        for h in range(Q_BLOCKS):
            qs = slice(h * P, (h + 1) * P)
            result = sb.tile([P, V_BLOCKS, P], F32, name=f"result{h}")
            accs = [bank_tile(acc_bank[h, b], [P, P], f"acc{h}{b}") for b in range(V_BLOCKS)]
            for b in range(V_BLOCKS):
                for g in range(SLOT_PASSES):
                    cols = slice((SLOT_PASSES * b + g) * P, (SLOT_PASSES * b + g + 1) * P)
                    nc.tensor.matmul_mx(
                        accs[b][:],
                        lhsT=w_codes[:, g, h].bitcast(FP8X4),
                        lhsT_scale=w_scales[:, g, h],
                        rhs=v_codes[:, cols].bitcast(FP8X4),
                        rhs_scale=v_scales[:, cols],
                        start=(g == 0),
                        stop=(g == SLOT_PASSES - 1),
                    )
            for b in range(V_BLOCKS):
                acc = accs[b]
                if (h, b) == (1, 1):
                    nc.vector.tensor_scalar_mul(result[:, b, :], acc[:], 1.0 / 16.0)
                else:
                    nc.scalar.activation(result[:, b, :], acc[:], ACT.Copy, scale=1.0 / 16.0)
            nc.sync.dma_start(out[0, qs, :], result[:].rearrange("q b e -> q (b e)"))
